import numpy as np
import ml_dtypes


def mxq(x, axis, fmt="e4m3"):
    dtype, down = {"e4m3": (ml_dtypes.float8_e4m3fn, 7), "e5m2": (ml_dtypes.float8_e5m2, 14)}[fmt]
    v = np.moveaxis(np.asarray(x, np.float32).astype(ml_dtypes.bfloat16).astype(np.float64), axis, -1)
    blocks = v.reshape(v.shape[:-1] + (-1, 32))
    amax = np.abs(blocks).max(-1, keepdims=True)
    byte = np.maximum(np.where(amax > 0, np.frexp(amax)[1] - 1 + 127, 0) - down, 1)
    scale = np.exp2(byte - 127.0)
    codes = (blocks / scale).astype(np.float32).astype(dtype).astype(np.float64)
    return np.moveaxis((codes * scale).reshape(v.shape), -1, axis)


WIDE = False


def mx_kscale(k):
    if not WIDE:
        return np.ones(k)
    levels = np.array([10, -10, 5, -5, 0])
    if k % 512:
        return np.exp2(np.random.permutation(np.resize(levels, k // 32))).repeat(32)
    a = np.empty((k // 512, 16))
    for p in range(k // 512):
        a[p, :8] = np.random.permutation(np.resize(levels, 8))
        for g in range(8):
            far = levels[np.abs(levels - a[p, g]) >= 10]
            a[p, g + 8] = far[np.random.randint(len(far))]
    return np.exp2(a.ravel()).repeat(32)


def f64(x):
    return np.asarray(x).astype(np.float64)


def striped(idx):
    return np.tile(idx.reshape(-1, 16).T, (8, 1)).astype(np.uint16)


def unstriped(offs):
    return offs[:16].T.reshape(-1).astype(np.int64)


def pack_weight(w):
    k, n = w.shape
    w = f64(np.asarray(w, np.float32).astype(ml_dtypes.bfloat16)).reshape(k // 32, 32, n)
    amax = np.abs(w).max(1)
    byte = np.clip(np.where(amax > 0, np.frexp(amax)[1] - 1 + 127 - 7, 1), 1, 254)
    scaled = (w * np.exp2(127.0 - byte)[:, None, :]).reshape(k, n).astype(np.float32)
    words = np.ascontiguousarray(scaled.reshape(k // 512, 128, 4, n).transpose(0, 1, 3, 2)).astype(ml_dtypes.float8_e4m3fn).view(np.uint8)
    return words, np.ascontiguousarray(byte.astype(np.uint8).reshape(k // 512, 16, n))


def unpack_weight(words, scales):
    g, p, n, _ = words.shape
    vals = np.ascontiguousarray(words).view(ml_dtypes.float8_e4m3fn).astype(np.float64) * np.repeat(np.exp2(scales.astype(np.float64) - 127.0), 8, axis=1)[..., None]
    return vals.transpose(0, 1, 3, 2).reshape(g * 512, n)


K, T, S, V, W = 512, 2048, 512, 512, 2048


def setup_inputs():
    n = np.random.standard_normal
    s = mx_kscale(K)[:, None]
    packed_xT = pack_weight(n((K, T)) * s)
    packed_eT = pack_weight(n((K, W)) / np.sqrt(2 * K) / s)
    packed_fT = pack_weight(n((K, W)) / np.sqrt(2 * K) / s)
    return {
        "x_words": packed_xT[0],
        "x_scales": packed_xT[1],
        "e_words": packed_eT[0],
        "e_scales": packed_eT[1],
        "f_words": packed_fT[0],
        "f_scales": packed_fT[1],
        "hT": (n((K, S)) * s).astype(np.float32),
        "offs": striped(np.random.permutation(T)[:S]),
        "cand": striped(np.random.permutation(W)[:V]),
    }


def reference(x_words, x_scales, e_words, e_scales, f_words, f_scales, hT, offs, cand):
    xq = unpack_weight(x_words, x_scales)[:, unstriped(offs)]
    e_cand = unpack_weight(e_words, e_scales)[:, unstriped(cand)]
    hTq = mxq(f64(hT), 0, "e4m3")
    f_cand = unpack_weight(f_words, f_scales)[:, unstriped(cand)]
    y = xq.T @ e_cand + hTq.T @ f_cand
    e = np.exp(y - y.max(axis=1, keepdims=True))
    return e / e.sum(axis=1, keepdims=True)

@@ -1,0 +1,126 @@
+from contextlib import ExitStack
+
+import concourse.mybir as mybir
+
+K, T, S, V = 512, 2048, 512, 512
+FLOPS = 2 * 2 * K * S * V
+
+F32 = mybir.dt.float32
+BF16 = mybir.dt.bfloat16
+I32 = mybir.dt.int32
+U32 = mybir.dt.uint32
+U16 = mybir.dt.uint16
+U8 = mybir.dt.uint8
+FP8X4 = mybir.dt.float8_e4m3fn_x4
+EXP = mybir.ActivationFunctionType.Exp
+ALU = mybir.AluOpType
+
+P = 128
+PACK = 4
+TILES = S // P
+E_ROW, X_ROW, F_ROW = 0, 4, 8
+
+
+def tile_picked_zsess_soft_p_kernel(tc, x_words, x_scales, e_words, e_scales, f_words, f_scales, hT, offs, cand, out):
+    nc = tc.nc
+    with ExitStack() as ctx:
+        keep = ctx.enter_context(tc.tile_pool(name="keep", bufs=1))
+        psum = ctx.enter_context(tc.psum_pool(name="psum", bufs=1))
+
+        def load_scales(queue, table, scales, first_row):
+            rows = scales[0].rearrange("(q r) c -> r q c", r=4)
+            for r in range(4):
+                queue.dma_start(out=table[first_row + r : P : 32, :].bitcast(I32), in_=rows[r].bitcast(I32))
+
+        def load_words(table, words):
+            nc.sync.dma_start(out=table[:], in_=words[0].rearrange("p n t -> p (n t)").bitcast(I32))
+
+        cand_list = keep.tile([P, V // 16], U16)
+        offs_list = keep.tile([P, S // 16], U16)
+        nc.sync.dma_start(cand_list[:], cand)
+        nc.sync.dma_start(offs_list[:], offs)
+
+        e_scale_table = keep.tile([P, T], U8, tag="es_then_f", align_bytes=64)
+        x_scale_table = keep.tile([P, T], U8, align_bytes=64)
+        f_scale_table = keep.tile([P, T], U8, align_bytes=64)
+        for table in (e_scale_table, x_scale_table, f_scale_table):
+            nc.vector.memset(table[:].bitcast(I32), 0)
+        warm_in = keep.tile([P, 1], F32)
+        warm_out = keep.tile([P, 1], F32)
+        nc.vector.memset(warm_in[:], 0.0)
+
+        e_word_table = keep.tile([P, T], I32, tag="e_then_h", align_bytes=64)
+        x_word_table = keep.tile([P, T], I32, align_bytes=64)
+        load_words(e_word_table, e_words)
+        load_scales(nc.scalar, e_scale_table, e_scales, E_ROW)
+        load_words(x_word_table, x_words)
+        load_scales(nc.gpsimd, x_scale_table, x_scales, X_ROW)
+        load_scales(nc.gpsimd, f_scale_table, f_scales, F_ROW)
+        nc.scalar.activation(warm_out[:], warm_in[:], EXP)
+
+        e_scale = keep.tile([P, V], U8, align_bytes=64)
+        x_scale = keep.tile([P, S], U8, align_bytes=64)
+        f_scale = keep.tile([P, V], U8, align_bytes=64)
+        e_code = keep.tile([P, V], U32, align_bytes=64)
+        x_code = keep.tile([P, S], U32, align_bytes=64)
+        f_code = keep.tile([P, V], U32, align_bytes=64)
+
+        nc.vector.tensor_copy(e_scale[:], e_scale_table[:].indirect(cand_list[:]))
+        f_word_table = keep.tile([P, T], I32, tag="es_then_f", align_bytes=64)
+        load_words(f_word_table, f_words)
+        nc.vector.tensor_copy(e_code[:], e_word_table[:].bitcast(U32).indirect(cand_list[:]))
+        h_raw = keep.tile([P, TILES, PACK, P], F32, tag="e_then_h", align_bytes=64)
+        h_view = hT.rearrange("(p j) (t c) -> t p j c", j=PACK, c=P)
+        for t in range(TILES):
+            nc.sync.dma_start(out=h_raw[:, t], in_=h_view[t])
+        nc.vector.tensor_copy(x_scale[:], x_scale_table[:].indirect(offs_list[:]))
+        nc.vector.tensor_copy(x_code[:], x_word_table[:].bitcast(U32).indirect(offs_list[:]))
+
+        scores = [psum.tile([P, V], F32, name=f"scores{t}") for t in range(TILES)]
+        for t in range(TILES):
+            users = slice(t * P, (t + 1) * P)
+            nc.tensor.matmul_mx(
+                out=scores[t][:],
+                lhsT=x_code[:, users].bitcast(FP8X4),
+                lhsT_scale=x_scale[X_ROW:, users],
+                rhs=e_code[:].bitcast(FP8X4),
+                rhs_scale=e_scale[E_ROW:, :],
+                start=True,
+                stop=False,
+            )
+
+        nc.vector.tensor_copy(f_scale[:], f_scale_table[:].indirect(cand_list[:]))
+        nc.vector.tensor_copy(f_code[:], f_word_table[:].bitcast(U32).indirect(cand_list[:]))
+
+        for t in range(TILES):
+            grouped = keep.tile([P, P, PACK], BF16, name=f"grouped{t}", align_bytes=64)
+            nc.scalar.copy(
+                out=grouped[:].rearrange("p (c i) j -> p c j i", i=4),
+                in_=h_raw[:, t].rearrange("p j (c i) -> p c j i", i=4),
+            )
+            h_code = keep.tile([P, P], U32, name=f"h_code{t}", align_bytes=64)
+            h_scale = keep.tile([P, P], U8, name=f"h_scale{t}", align_bytes=64)
+            nc.vector.quantize_mx(
+                out=h_code[:].bitcast(FP8X4), scales=h_scale[:], in_=grouped[:].rearrange("p c j -> p (c j)")
+            )
+            nc.tensor.matmul_mx(
+                out=scores[t][:],
+                lhsT=h_code[:].bitcast(FP8X4),
+                lhsT_scale=h_scale[:],
+                rhs=f_code[:].bitcast(FP8X4),
+                rhs_scale=f_scale[F_ROW:, :],
+                start=False,
+                stop=True,
+            )
+
+        for t in range(TILES):
+            neg_max = keep.tile([P, 1], F32, name=f"neg_max{t}")
+            total = keep.tile([P, 1], F32, name=f"total{t}")
+            inverse = keep.tile([P, 1], F32, name=f"inverse{t}")
+            weights = keep.tile([P, V], F32, name=f"weights{t}")
+            probs = keep.tile([P, V], F32, name=f"probs{t}")
+            nc.vector.tensor_reduce(neg_max[:], scores[t][:], mybir.AxisListType.X, ALU.max, negate=True)
+            nc.scalar.activation(weights[:], scores[t][:], EXP, bias=neg_max[:], accum_out=total[:])
+            nc.vector.reciprocal(inverse[:], total[:])
+            nc.vector.tensor_scalar(probs[:], weights[:], inverse[:], None, ALU.mult)
+            nc.sync.dma_start(out=out[t * P : (t + 1) * P, :], in_=probs[:])

@@ -18,7 +18,8 @@ ALU = mybir.AluOpType
 P = 128
 PACK = 4
 TILES = S // P
-E_ROW, X_ROW, F_ROW = 0, 4, 8
+ROW_STEP = 8
+EARLY = 3
 
 
 def tile_picked_zsess_soft_p_kernel(tc, x_words, x_scales, e_words, e_scales, f_words, f_scales, hT, offs, cand, out):
@@ -27,100 +28,129 @@ def tile_picked_zsess_soft_p_kernel(tc, x_words, x_scales, e_words, e_scales, f_
         keep = ctx.enter_context(tc.tile_pool(name="keep", bufs=1))
         psum = ctx.enter_context(tc.psum_pool(name="psum", bufs=1))
 
-        def load_scales(queue, table, scales, first_row):
-            rows = scales[0].rearrange("(q r) c -> r q c", r=4)
-            for r in range(4):
-                queue.dma_start(out=table[first_row + r : P : 32, :].bitcast(I32), in_=rows[r].bitcast(I32))
+        def sbuf(shape, dtype, name, tag=None):
+            return keep.tile(shape, dtype, name=name, tag=tag or name, align_bytes=64)
+
+        def load_scales(table, scales):
+            nc.scalar.dma_start(out=table[0:P:ROW_STEP, :].bitcast(I32), in_=scales[0].bitcast(I32))
 
         def load_words(table, words):
             nc.sync.dma_start(out=table[:], in_=words[0].rearrange("p n t -> p (n t)").bitcast(I32))
+
+        def gather_words(picked_words, table, entries):
+            nc.vector.tensor_copy(picked_words, table[:].bitcast(U32).indirect(entries))
+
+        h_rows = hT.rearrange("(p j) c -> p j c", j=PACK)
+
+        def interleave(raw, width, name):
+            grouped = sbuf([P, width, PACK], BF16, name)
+            nc.scalar.copy(
+                out=grouped[:].rearrange("p (c i) j -> p c j i", i=4),
+                in_=raw.rearrange("p j (c i) -> p c j i", i=4),
+            )
+            return grouped
+
+        def quantize(grouped, codes, scales):
+            nc.vector.quantize_mx(out=codes.bitcast(FP8X4), scales=scales, in_=grouped[:].rearrange("p c j -> p (c j)"))
 
         cand_list = keep.tile([P, V // 16], U16)
         offs_list = keep.tile([P, S // 16], U16)
         nc.sync.dma_start(cand_list[:], cand)
         nc.sync.dma_start(offs_list[:], offs)
 
-        e_scale_table = keep.tile([P, T], U8, tag="es_then_f", align_bytes=64)
-        x_scale_table = keep.tile([P, T], U8, align_bytes=64)
-        f_scale_table = keep.tile([P, T], U8, align_bytes=64)
+        e_scale_table = sbuf([P, T], U8, "e_scale_table", "es_then_e")
+        x_scale_table = sbuf([P, T], U8, "x_scale_table", "xs_then_x")
+        f_scale_table = sbuf([P, T], U8, "f_scale_table", "fs_then_h")
         for table in (e_scale_table, x_scale_table, f_scale_table):
             nc.vector.memset(table[:].bitcast(I32), 0)
-        warm_in = keep.tile([P, 1], F32)
-        warm_out = keep.tile([P, 1], F32)
+        warm_in = sbuf([P, 1], F32, "warm_in")
+        warm_out = sbuf([P, 1], F32, "warm_out")
         nc.vector.memset(warm_in[:], 0.0)
 
-        e_word_table = keep.tile([P, T], I32, tag="e_then_h", align_bytes=64)
-        x_word_table = keep.tile([P, T], I32, align_bytes=64)
-        load_words(e_word_table, e_words)
-        load_scales(nc.scalar, e_scale_table, e_scales, E_ROW)
-        load_words(x_word_table, x_words)
-        load_scales(nc.gpsimd, x_scale_table, x_scales, X_ROW)
-        load_scales(nc.gpsimd, f_scale_table, f_scales, F_ROW)
-        nc.scalar.activation(warm_out[:], warm_in[:], EXP)
-
-        e_scale = keep.tile([P, V], U8, align_bytes=64)
-        x_scale = keep.tile([P, S], U8, align_bytes=64)
-        f_scale = keep.tile([P, V], U8, align_bytes=64)
-        e_code = keep.tile([P, V], U32, align_bytes=64)
-        x_code = keep.tile([P, S], U32, align_bytes=64)
-        f_code = keep.tile([P, V], U32, align_bytes=64)
-
-        nc.vector.tensor_copy(e_scale[:], e_scale_table[:].indirect(cand_list[:]))
-        f_word_table = keep.tile([P, T], I32, tag="es_then_f", align_bytes=64)
+        h_early = sbuf([P, PACK, EARLY * P], F32, "h_early", "h_then_planes")
+        nc.sync.dma_start(out=h_early[:], in_=h_rows[:, :, : EARLY * P])
+        f_word_table = sbuf([P, T], I32, "f_word_table")
         load_words(f_word_table, f_words)
-        nc.vector.tensor_copy(e_code[:], e_word_table[:].bitcast(U32).indirect(cand_list[:]))
-        h_raw = keep.tile([P, TILES, PACK, P], F32, tag="e_then_h", align_bytes=64)
-        h_view = hT.rearrange("(p j) (t c) -> t p j c", j=PACK, c=P)
-        for t in range(TILES):
-            nc.sync.dma_start(out=h_raw[:, t], in_=h_view[t])
-        nc.vector.tensor_copy(x_scale[:], x_scale_table[:].indirect(offs_list[:]))
-        nc.vector.tensor_copy(x_code[:], x_word_table[:].bitcast(U32).indirect(offs_list[:]))
+        load_scales(e_scale_table, e_scales)
+        load_scales(x_scale_table, x_scales)
+        load_scales(f_scale_table, f_scales)
+        nc.scalar.activation(warm_out[:], warm_in[:], EXP)
+        grouped = [interleave(h_early[:, :, t * P : (t + 1) * P], P, f"grouped{t}") for t in range(EARLY)]
 
+        planes = sbuf([P, 3 * V], U8, "planes", "h_then_planes")
+        nc.gpsimd.memset(planes[:].bitcast(I32), 0)
+        picked = sbuf([P, 3 * V], U8, "picked")
+        e_cols, x_cols, f_cols = slice(0, V), slice(V, V + S), slice(V + S, 2 * V + S)
+        nc.vector.tensor_copy(picked[:, e_cols], e_scale_table[:].indirect(cand_list[:]))
+        e_word_table = sbuf([P, T], I32, "e_word_table", "es_then_e")
+        load_words(e_word_table, e_words)
+        nc.vector.tensor_copy(picked[:, x_cols], x_scale_table[:].indirect(offs_list[:]))
+        x_word_table = sbuf([P, T], I32, "x_word_table", "xs_then_x")
+        load_words(x_word_table, x_words)
+        nc.vector.tensor_copy(picked[:, f_cols], f_scale_table[:].indirect(cand_list[:]))
+        for r in range(4):
+            nc.scalar.dma_start(out=planes[r:P:32, :].bitcast(I32), in_=picked[ROW_STEP * r : P : 32, :].bitcast(I32))
+        h_late = sbuf([P, TILES - EARLY, PACK, P], F32, "h_late", "fs_then_h")
+        for t in range(EARLY, TILES):
+            nc.sync.dma_start(out=h_late[:, t - EARLY], in_=h_rows[:, :, t * P : (t + 1) * P])
+
+        f_code = sbuf([P, V], U32, "f_code")
+        gather_words(f_code[:], f_word_table, cand_list[:])
+        h_code = sbuf([P, S], U32, "h_code")
+        h_scale = sbuf([P, S], U8, "h_scale")
         scores = [psum.tile([P, V], F32, name=f"scores{t}") for t in range(TILES)]
-        for t in range(TILES):
+        e_code = sbuf([P, V], U32, "e_code")
+        x_code = sbuf([P, S], U32, "x_code")
+
+        def session_pass(t, first):
+            users = slice(t * P, (t + 1) * P)
+            nc.tensor.matmul_mx(
+                out=scores[t][:],
+                lhsT=h_code[:, users].bitcast(FP8X4),
+                lhsT_scale=h_scale[:, users],
+                rhs=f_code[:].bitcast(FP8X4),
+                rhs_scale=planes[:, f_cols],
+                start=first,
+                stop=not first,
+            )
+
+        def user_pass(t, first):
             users = slice(t * P, (t + 1) * P)
             nc.tensor.matmul_mx(
                 out=scores[t][:],
                 lhsT=x_code[:, users].bitcast(FP8X4),
-                lhsT_scale=x_scale[X_ROW:, users],
+                lhsT_scale=planes[:, V + t * P : V + (t + 1) * P],
                 rhs=e_code[:].bitcast(FP8X4),
-                rhs_scale=e_scale[E_ROW:, :],
-                start=True,
-                stop=False,
+                rhs_scale=planes[:, e_cols],
+                start=first,
+                stop=not first,
             )
 
-        nc.vector.tensor_copy(f_scale[:], f_scale_table[:].indirect(cand_list[:]))
-        nc.vector.tensor_copy(f_code[:], f_word_table[:].bitcast(U32).indirect(cand_list[:]))
+        for t in range(EARLY):
+            quantize(grouped[t], h_code[:, t * P : (t + 1) * P], h_scale[:, t * P : (t + 1) * P])
+        for t in range(EARLY):
+            session_pass(t, True)
+        gather_words(e_code[:], e_word_table, cand_list[:])
+        for u in range(2):
+            gather_words(x_code[:, u * 256 : (u + 1) * 256], x_word_table, offs_list[:, u * 16 : (u + 1) * 16])
+        for t in range(TILES):
+            user_pass(t, t >= EARLY)
+        for t in range(EARLY, TILES):
+            late = interleave(h_late[:, t - EARLY], P, f"grouped{t}")
+            quantize(late, h_code[:, t * P : (t + 1) * P], h_scale[:, t * P : (t + 1) * P])
+            session_pass(t, False)
 
         for t in range(TILES):
-            grouped = keep.tile([P, P, PACK], BF16, name=f"grouped{t}", align_bytes=64)
-            nc.scalar.copy(
-                out=grouped[:].rearrange("p (c i) j -> p c j i", i=4),
-                in_=h_raw[:, t].rearrange("p j (c i) -> p c j i", i=4),
-            )
-            h_code = keep.tile([P, P], U32, name=f"h_code{t}", align_bytes=64)
-            h_scale = keep.tile([P, P], U8, name=f"h_scale{t}", align_bytes=64)
-            nc.vector.quantize_mx(
-                out=h_code[:].bitcast(FP8X4), scales=h_scale[:], in_=grouped[:].rearrange("p c j -> p (c j)")
-            )
-            nc.tensor.matmul_mx(
-                out=scores[t][:],
-                lhsT=h_code[:].bitcast(FP8X4),
-                lhsT_scale=h_scale[:],
-                rhs=f_code[:].bitcast(FP8X4),
-                rhs_scale=f_scale[F_ROW:, :],
-                start=False,
-                stop=True,
-            )
-
-        for t in range(TILES):
-            neg_max = keep.tile([P, 1], F32, name=f"neg_max{t}")
-            total = keep.tile([P, 1], F32, name=f"total{t}")
-            inverse = keep.tile([P, 1], F32, name=f"inverse{t}")
-            weights = keep.tile([P, V], F32, name=f"weights{t}")
-            probs = keep.tile([P, V], F32, name=f"probs{t}")
+            neg_max = sbuf([P, 1], F32, f"neg_max{t}")
+            total = sbuf([P, 1], F32, f"total{t}")
+            inverse = sbuf([P, 1], F32, f"inverse{t}")
+            weights = sbuf([P, V], F32, f"weights{t}")
+            probs = sbuf([P, V], F32, f"probs{t}")
             nc.vector.tensor_reduce(neg_max[:], scores[t][:], mybir.AxisListType.X, ALU.max, negate=True)
             nc.scalar.activation(weights[:], scores[t][:], EXP, bias=neg_max[:], accum_out=total[:])
             nc.vector.reciprocal(inverse[:], total[:])
-            nc.vector.tensor_scalar(probs[:], weights[:], inverse[:], None, ALU.mult)
+            if t < 2:
+                nc.gpsimd.tensor_scalar(probs[:], weights[:], inverse[:], 1.0, ALU.mult, ALU.mult)
+            else:
+                nc.vector.tensor_scalar(probs[:], weights[:], inverse[:], None, ALU.mult)
             nc.sync.dma_start(out=out[t * P : (t + 1) * P, :], in_=probs[:])

@@ -13,13 +13,16 @@ U16 = mybir.dt.uint16
 U8 = mybir.dt.uint8
 FP8X4 = mybir.dt.float8_e4m3fn_x4
 EXP = mybir.ActivationFunctionType.Exp
+COPY = mybir.ActivationFunctionType.Copy
 ALU = mybir.AluOpType
 
 P = 128
 PACK = 4
 TILES = S // P
 ROW_STEP = 8
-EARLY = 3
+HALF = S // 2
+FILL = 512
+LAST_SPLIT = 320
 
 
 def tile_picked_zsess_soft_p_kernel(tc, x_words, x_scales, e_words, e_scales, f_words, f_scales, hT, offs, cand, out):
@@ -32,77 +35,70 @@ def tile_picked_zsess_soft_p_kernel(tc, x_words, x_scales, e_words, e_scales, f_
             return keep.tile(shape, dtype, name=name, tag=tag or name, align_bytes=64)
 
         def load_scales(table, scales):
-            nc.scalar.dma_start(out=table[0:P:ROW_STEP, :].bitcast(I32), in_=scales[0].bitcast(I32))
+            nc.sync.dma_start(out=table[0:P:ROW_STEP, :].bitcast(I32), in_=scales[0].bitcast(I32))
 
-        def load_words(table, words):
-            nc.sync.dma_start(out=table[:], in_=words[0].rearrange("p n t -> p (n t)").bitcast(I32))
+        def load_words(table, words, cols):
+            nc.sync.dma_start(out=table[:, cols], in_=words[0].rearrange("p n t -> p (n t)").bitcast(I32)[:, cols])
 
         def gather_words(picked_words, table, entries):
             nc.vector.tensor_copy(picked_words, table[:].bitcast(U32).indirect(entries))
 
-        h_rows = hT.rearrange("(p j) c -> p j c", j=PACK)
-
-        def interleave(raw, width, name):
-            grouped = sbuf([P, width, PACK], BF16, name)
-            nc.scalar.copy(
-                out=grouped[:].rearrange("p (c i) j -> p c j i", i=4),
-                in_=raw.rearrange("p j (c i) -> p c j i", i=4),
-            )
-            return grouped
-
-        def quantize(grouped, codes, scales):
-            nc.vector.quantize_mx(out=codes.bitcast(FP8X4), scales=scales, in_=grouped[:].rearrange("p c j -> p (c j)"))
-
         cand_list = keep.tile([P, V // 16], U16)
         offs_list = keep.tile([P, S // 16], U16)
-        nc.sync.dma_start(cand_list[:], cand)
-        nc.sync.dma_start(offs_list[:], offs)
 
-        e_scale_table = sbuf([P, T], U8, "e_scale_table", "es_then_e")
-        x_scale_table = sbuf([P, T], U8, "x_scale_table", "xs_then_x")
-        f_scale_table = sbuf([P, T], U8, "f_scale_table", "fs_then_h")
-        for table in (e_scale_table, x_scale_table, f_scale_table):
-            nc.vector.memset(table[:].bitcast(I32), 0)
+        e_scale_table = sbuf([P, T], U8, "e_scale_table")
+        x_scale_table = sbuf([P, T], U8, "x_scale_table")
+        f_scale_table = sbuf([P, T], U8, "f_scale_table", "f_scales_then_h_codes")
+        planes = sbuf([P, 3 * V], U8, "planes")
         warm_in = sbuf([P, 1], F32, "warm_in")
         warm_out = sbuf([P, 1], F32, "warm_out")
+        for table in (e_scale_table, x_scale_table, f_scale_table):
+            nc.vector.memset(table[:].bitcast(I32), 0)
         nc.vector.memset(warm_in[:], 0.0)
-
-        h_early = sbuf([P, PACK, EARLY * P], F32, "h_early", "h_then_planes")
-        nc.sync.dma_start(out=h_early[:], in_=h_rows[:, :, : EARLY * P])
-        f_word_table = sbuf([P, T], I32, "f_word_table")
-        load_words(f_word_table, f_words)
-        load_scales(e_scale_table, e_scales)
-        load_scales(x_scale_table, x_scales)
-        load_scales(f_scale_table, f_scales)
         nc.scalar.activation(warm_out[:], warm_in[:], EXP)
-        grouped = [interleave(h_early[:, :, t * P : (t + 1) * P], P, f"grouped{t}") for t in range(EARLY)]
+        nc.vector.memset(planes[:].bitcast(I32), 0)
 
-        planes = sbuf([P, 3 * V], U8, "planes", "h_then_planes")
-        nc.gpsimd.memset(planes[:].bitcast(I32), 0)
+        f_word_table = sbuf([P, T], I32, "f_word_table")
+        e_word_table = sbuf([P, T], I32, "e_word_table")
+        x_word_table = sbuf([P, T], I32, "x_word_table")
+        h_raw = sbuf([P, PACK, S], F32, "h_raw", "h_raw_then_e_codes")
+        load_words(f_word_table, f_words, slice(0, FILL))
+        nc.sync.dma_start(cand_list[:], cand)
+        load_scales(e_scale_table, e_scales)
+        load_words(f_word_table, f_words, slice(FILL, 2 * FILL))
+        load_scales(x_scale_table, x_scales)
+        nc.sync.dma_start(offs_list[:], offs)
+        load_scales(f_scale_table, f_scales)
+        nc.sync.dma_start(out=h_raw[:], in_=hT.rearrange("(p j) c -> p j c", j=PACK))
+        load_words(f_word_table, f_words, slice(2 * FILL, T))
+        load_words(e_word_table, e_words, slice(0, T))
+
         picked = sbuf([P, 3 * V], U8, "picked")
         e_cols, x_cols, f_cols = slice(0, V), slice(V, V + S), slice(V + S, 2 * V + S)
         nc.vector.tensor_copy(picked[:, e_cols], e_scale_table[:].indirect(cand_list[:]))
-        e_word_table = sbuf([P, T], I32, "e_word_table", "es_then_e")
-        load_words(e_word_table, e_words)
         nc.vector.tensor_copy(picked[:, x_cols], x_scale_table[:].indirect(offs_list[:]))
-        x_word_table = sbuf([P, T], I32, "x_word_table", "xs_then_x")
-        load_words(x_word_table, x_words)
         nc.vector.tensor_copy(picked[:, f_cols], f_scale_table[:].indirect(cand_list[:]))
         for r in range(4):
-            nc.scalar.dma_start(out=planes[r:P:32, :].bitcast(I32), in_=picked[ROW_STEP * r : P : 32, :].bitcast(I32))
-        h_late = sbuf([P, TILES - EARLY, PACK, P], F32, "h_late", "fs_then_h")
-        for t in range(EARLY, TILES):
-            nc.sync.dma_start(out=h_late[:, t - EARLY], in_=h_rows[:, :, t * P : (t + 1) * P])
+            nc.sync.dma_start(out=planes[r:P:32, :].bitcast(I32), in_=picked[ROW_STEP * r : P : 32, :].bitcast(I32))
+        load_words(x_word_table, x_words, slice(0, T))
 
         f_code = sbuf([P, V], U32, "f_code")
-        gather_words(f_code[:], f_word_table, cand_list[:])
-        h_code = sbuf([P, S], U32, "h_code")
-        h_scale = sbuf([P, S], U8, "h_scale")
-        scores = [psum.tile([P, V], F32, name=f"scores{t}") for t in range(TILES)]
-        e_code = sbuf([P, V], U32, "e_code")
         x_code = sbuf([P, S], U32, "x_code")
+        h_code = sbuf([P, S], U32, "h_code", "f_scales_then_h_codes")
+        h_scale = sbuf([P, S], U8, "h_scale")
+        gather_words(f_code[:], f_word_table, cand_list[:])
+        for u in range(2):
+            users = slice(u * HALF, (u + 1) * HALF)
+            grouped = sbuf([P, HALF, PACK], BF16, f"grouped{u}")
+            nc.scalar.copy(out=grouped[:], in_=h_raw[:, :, users].rearrange("p j c -> p c j"))
+            nc.vector.quantize_mx(
+                out=h_code[:, users].bitcast(FP8X4),
+                scales=h_scale[:, users],
+                in_=grouped[:].rearrange("p c j -> p (c j)"),
+            )
 
-        def session_pass(t, first):
+        scores = [psum.tile([P, V], F32, name=f"scores{t}") for t in range(TILES)]
+        for t in range(TILES):
             users = slice(t * P, (t + 1) * P)
             nc.tensor.matmul_mx(
                 out=scores[t][:],
@@ -110,47 +106,54 @@ def tile_picked_zsess_soft_p_kernel(tc, x_words, x_scales, e_words, e_scales, f_
                 lhsT_scale=h_scale[:, users],
                 rhs=f_code[:].bitcast(FP8X4),
                 rhs_scale=planes[:, f_cols],
-                start=first,
-                stop=not first,
+                start=True,
+                stop=False,
             )
-
-        def user_pass(t, first):
-            users = slice(t * P, (t + 1) * P)
+        e_code = sbuf([P, V], U32, "e_code", "h_raw_then_e_codes")
+        gather_words(e_code[:], e_word_table, cand_list[:])
+        for u in range(2):
+            gather_words(x_code[:, u * HALF : (u + 1) * HALF], x_word_table, offs_list[:, u * HALF // 16 : (u + 1) * HALF // 16])
+        for t in range(TILES):
             nc.tensor.matmul_mx(
                 out=scores[t][:],
-                lhsT=x_code[:, users].bitcast(FP8X4),
+                lhsT=x_code[:, t * P : (t + 1) * P].bitcast(FP8X4),
                 lhsT_scale=planes[:, V + t * P : V + (t + 1) * P],
                 rhs=e_code[:].bitcast(FP8X4),
                 rhs_scale=planes[:, e_cols],
-                start=first,
-                stop=not first,
+                start=False,
+                stop=True,
             )
 
-        for t in range(EARLY):
-            quantize(grouped[t], h_code[:, t * P : (t + 1) * P], h_scale[:, t * P : (t + 1) * P])
-        for t in range(EARLY):
-            session_pass(t, True)
-        gather_words(e_code[:], e_word_table, cand_list[:])
-        for u in range(2):
-            gather_words(x_code[:, u * 256 : (u + 1) * 256], x_word_table, offs_list[:, u * 16 : (u + 1) * 16])
-        for t in range(TILES):
-            user_pass(t, t >= EARLY)
-        for t in range(EARLY, TILES):
-            late = interleave(h_late[:, t - EARLY], P, f"grouped{t}")
-            quantize(late, h_code[:, t * P : (t + 1) * P], h_scale[:, t * P : (t + 1) * P])
-            session_pass(t, False)
+        weights = [sbuf([P, V], F32, f"weights{t}") for t in range(TILES)]
+        totals = [sbuf([P, 1], F32, f"total{t}") for t in range(TILES)]
 
-        for t in range(TILES):
-            neg_max = sbuf([P, 1], F32, f"neg_max{t}")
-            total = sbuf([P, 1], F32, f"total{t}")
-            inverse = sbuf([P, 1], F32, f"inverse{t}")
-            weights = sbuf([P, V], F32, f"weights{t}")
-            probs = sbuf([P, V], F32, f"probs{t}")
+        def exponentials(t):
+            neg_max = sbuf([P, 1], F32, f"neg_max{t}", "neg_max0" if t == 2 else None)
             nc.vector.tensor_reduce(neg_max[:], scores[t][:], mybir.AxisListType.X, ALU.max, negate=True)
-            nc.scalar.activation(weights[:], scores[t][:], EXP, bias=neg_max[:], accum_out=total[:])
-            nc.vector.reciprocal(inverse[:], total[:])
-            if t < 2:
-                nc.gpsimd.tensor_scalar(probs[:], weights[:], inverse[:], 1.0, ALU.mult, ALU.mult)
+            nc.scalar.activation(weights[t][:], scores[t][:], EXP, bias=neg_max[:], accum_out=totals[t][:])
+
+        def normalise(t):
+            rows = slice(t * P, (t + 1) * P)
+            inverse = sbuf([P, 1], F32, f"inverse{t}")
+            probs = sbuf([P, V], F32, f"probs{t}")
+            nc.vector.reciprocal(inverse[:], totals[t][:])
+            if t == 0:
+                nc.gpsimd.tensor_scalar(probs[:], weights[t][:], inverse[:], 1.0, ALU.mult, ALU.mult)
+                nc.sync.dma_start(out=out[rows, :], in_=probs[:])
+            elif t < TILES - 1:
+                nc.vector.tensor_scalar(probs[:], weights[t][:], inverse[:], None, ALU.mult)
+                nc.sync.dma_start(out=out[rows, :], in_=probs[:])
             else:
-                nc.vector.tensor_scalar(probs[:], weights[:], inverse[:], None, ALU.mult)
-            nc.sync.dma_start(out=out[t * P : (t + 1) * P, :], in_=probs[:])
+                left, right = slice(0, LAST_SPLIT), slice(LAST_SPLIT, V)
+                nc.vector.tensor_scalar(probs[:, left], weights[t][:, left], inverse[:], None, ALU.mult)
+                nc.sync.dma_start(out=out[rows, left], in_=probs[:, left])
+                nc.scalar.activation(probs[:, right], weights[t][:, right], COPY, scale=inverse[:])
+                nc.scalar.dma_start(out=out[rows, right], in_=probs[:, right])
+
+        exponentials(0)
+        exponentials(1)
+        normalise(0)
+        exponentials(2)
+        exponentials(3)
+        for t in range(1, TILES):
+            normalise(t)

@@ -47,16 +47,18 @@ def tile_picked_zsess_soft_p_kernel(tc, x_words, x_scales, e_words, e_scales, f_
         offs_list = keep.tile([P, S // 16], U16)
 
         e_scale_table = sbuf([P, T], U8, "e_scale_table")
-        x_scale_table = sbuf([P, T], U8, "x_scale_table")
-        f_scale_table = sbuf([P, T], U8, "f_scale_table", "f_scales_then_h_codes")
-        planes = sbuf([P, 3 * V], U8, "planes")
+        x_scale_table = sbuf([P, T], U8, "x_scale_table", "x_scales_then_h_codes")
+        f_scale_table = sbuf([P, T], U8, "f_scale_table")
+        f_plane = sbuf([P, V], U8, "f_plane")
+        ex_planes = sbuf([P, V + S], U8, "ex_planes")
         warm_in = sbuf([P, 1], F32, "warm_in")
         warm_out = sbuf([P, 1], F32, "warm_out")
-        for table in (e_scale_table, x_scale_table, f_scale_table):
+        for table in (f_scale_table, e_scale_table, x_scale_table):
             nc.vector.memset(table[:].bitcast(I32), 0)
         nc.vector.memset(warm_in[:], 0.0)
         nc.scalar.activation(warm_out[:], warm_in[:], EXP)
-        nc.vector.memset(planes[:].bitcast(I32), 0)
+        nc.vector.memset(f_plane[:].bitcast(I32), 0)
+        nc.vector.memset(ex_planes[:].bitcast(I32), 0)
 
         f_word_table = sbuf([P, T], I32, "f_word_table")
         e_word_table = sbuf([P, T], I32, "e_word_table")
@@ -64,27 +66,34 @@ def tile_picked_zsess_soft_p_kernel(tc, x_words, x_scales, e_words, e_scales, f_
         h_raw = sbuf([P, PACK, S], F32, "h_raw", "h_raw_then_e_codes")
         load_words(f_word_table, f_words, slice(0, FILL))
         nc.sync.dma_start(cand_list[:], cand)
-        load_scales(e_scale_table, e_scales)
-        load_words(f_word_table, f_words, slice(FILL, 2 * FILL))
-        load_scales(x_scale_table, x_scales)
-        nc.sync.dma_start(offs_list[:], offs)
         load_scales(f_scale_table, f_scales)
+        load_words(f_word_table, f_words, slice(FILL, 2 * FILL))
+        load_scales(e_scale_table, e_scales)
+        nc.sync.dma_start(offs_list[:], offs)
+        load_scales(x_scale_table, x_scales)
         nc.sync.dma_start(out=h_raw[:], in_=hT.rearrange("(p j) c -> p j c", j=PACK))
         load_words(f_word_table, f_words, slice(2 * FILL, T))
         load_words(e_word_table, e_words, slice(0, T))
 
         picked = sbuf([P, 3 * V], U8, "picked")
         e_cols, x_cols, f_cols = slice(0, V), slice(V, V + S), slice(V + S, 2 * V + S)
+
+        def move_scale_rows(planes, cols):
+            for r in range(4):
+                nc.sync.dma_start(
+                    out=planes[r:P:32, :].bitcast(I32), in_=picked[ROW_STEP * r : P : 32, cols].bitcast(I32)
+                )
+
+        nc.vector.tensor_copy(picked[:, f_cols], f_scale_table[:].indirect(cand_list[:]))
         nc.vector.tensor_copy(picked[:, e_cols], e_scale_table[:].indirect(cand_list[:]))
         nc.vector.tensor_copy(picked[:, x_cols], x_scale_table[:].indirect(offs_list[:]))
-        nc.vector.tensor_copy(picked[:, f_cols], f_scale_table[:].indirect(cand_list[:]))
-        for r in range(4):
-            nc.sync.dma_start(out=planes[r:P:32, :].bitcast(I32), in_=picked[ROW_STEP * r : P : 32, :].bitcast(I32))
+        move_scale_rows(f_plane, f_cols)
         load_words(x_word_table, x_words, slice(0, T))
+        move_scale_rows(ex_planes, slice(0, V + S))
 
         f_code = sbuf([P, V], U32, "f_code")
         x_code = sbuf([P, S], U32, "x_code")
-        h_code = sbuf([P, S], U32, "h_code", "f_scales_then_h_codes")
+        h_code = sbuf([P, S], U32, "h_code", "x_scales_then_h_codes")
         h_scale = sbuf([P, S], U8, "h_scale")
         gather_words(f_code[:], f_word_table, cand_list[:])
         for u in range(2):
@@ -105,7 +114,7 @@ def tile_picked_zsess_soft_p_kernel(tc, x_words, x_scales, e_words, e_scales, f_
                 lhsT=h_code[:, users].bitcast(FP8X4),
                 lhsT_scale=h_scale[:, users],
                 rhs=f_code[:].bitcast(FP8X4),
-                rhs_scale=planes[:, f_cols],
+                rhs_scale=f_plane[:],
                 start=True,
                 stop=False,
             )
@@ -117,9 +126,9 @@ def tile_picked_zsess_soft_p_kernel(tc, x_words, x_scales, e_words, e_scales, f_
             nc.tensor.matmul_mx(
                 out=scores[t][:],
                 lhsT=x_code[:, t * P : (t + 1) * P].bitcast(FP8X4),
-                lhsT_scale=planes[:, V + t * P : V + (t + 1) * P],
+                lhsT_scale=ex_planes[:, V + t * P : V + (t + 1) * P],
                 rhs=e_code[:].bitcast(FP8X4),
-                rhs_scale=planes[:, e_cols],
+                rhs_scale=ex_planes[:, e_cols],
                 start=False,
                 stop=True,
             )

@@ -19,9 +19,8 @@ ALU = mybir.AluOpType
 P = 128
 PACK = 4
 TILES = S // P
-ROW_STEP = 8
 HALF = S // 2
-FILL = 512
+FIRST_PIECE = 512
 LAST_SPLIT = 320
 
 
@@ -29,13 +28,17 @@ def tile_picked_zsess_soft_p_kernel(tc, x_words, x_scales, e_words, e_scales, f_
     nc = tc.nc
     with ExitStack() as ctx:
         keep = ctx.enter_context(tc.tile_pool(name="keep", bufs=1))
+        reuse = ctx.enter_context(tc.tile_pool(name="reuse", bufs=1))
         psum = ctx.enter_context(tc.psum_pool(name="psum", bufs=1))
 
         def sbuf(shape, dtype, name, tag=None):
             return keep.tile(shape, dtype, name=name, tag=tag or name, align_bytes=64)
 
+        def placed(shape, dtype, name, offset):
+            return reuse.tile(shape, dtype, name=name, tag=name, align_bytes=64, offset=offset)
+
         def load_scales(table, scales):
-            nc.sync.dma_start(out=table[0:P:ROW_STEP, :].bitcast(I32), in_=scales[0].bitcast(I32))
+            nc.sync.dma_start(out=table[32:96:4, :].bitcast(I32), in_=scales[0].bitcast(I32))
 
         def load_words(table, words, cols):
             nc.sync.dma_start(out=table[:, cols], in_=words[0].rearrange("p n t -> p (n t)").bitcast(I32)[:, cols])
@@ -46,9 +49,9 @@ def tile_picked_zsess_soft_p_kernel(tc, x_words, x_scales, e_words, e_scales, f_
         cand_list = keep.tile([P, V // 16], U16)
         offs_list = keep.tile([P, S // 16], U16)
 
-        e_scale_table = sbuf([P, T], U8, "e_scale_table")
-        x_scale_table = sbuf([P, T], U8, "x_scale_table", "x_scales_then_h_codes")
         f_scale_table = sbuf([P, T], U8, "f_scale_table")
+        e_scale_table = sbuf([P, T], U8, "e_scale_table")
+        x_scale_table = placed([P, T], U8, "x_scale_table", 1024)
         f_plane = sbuf([P, V], U8, "f_plane")
         ex_planes = sbuf([P, V + S], U8, "ex_planes")
         warm_in = sbuf([P, 1], F32, "warm_in")
@@ -62,92 +65,98 @@ def tile_picked_zsess_soft_p_kernel(tc, x_words, x_scales, e_words, e_scales, f_
 
         f_word_table = sbuf([P, T], I32, "f_word_table")
         e_word_table = sbuf([P, T], I32, "e_word_table")
-        x_word_table = sbuf([P, T], I32, "x_word_table")
-        h_raw = sbuf([P, PACK, S], F32, "h_raw", "h_raw_then_e_codes")
-        load_words(f_word_table, f_words, slice(0, FILL))
+        h_rows = hT.rearrange("(p j) c -> p j c", j=PACK)
+        h_pieces = [slice(0, HALF), slice(HALF, HALF + P), slice(HALF + P, S)]
+        h_early = sbuf([P, PACK, HALF], F32, "h_early")
+        h_raw = [h_early[:]]
+
+        def load_h(i):
+            nc.sync.dma_start(out=h_raw[i], in_=h_rows[:, :, h_pieces[i]])
+
         nc.sync.dma_start(cand_list[:], cand)
+        load_words(e_word_table, e_words, slice(0, FIRST_PIECE))
         load_scales(f_scale_table, f_scales)
-        load_words(f_word_table, f_words, slice(FILL, 2 * FILL))
+        load_h(0)
         load_scales(e_scale_table, e_scales)
         nc.sync.dma_start(offs_list[:], offs)
         load_scales(x_scale_table, x_scales)
-        nc.sync.dma_start(out=h_raw[:], in_=hT.rearrange("(p j) c -> p j c", j=PACK))
-        load_words(f_word_table, f_words, slice(2 * FILL, T))
-        load_words(e_word_table, e_words, slice(0, T))
+        load_words(e_word_table, e_words, slice(FIRST_PIECE, T))
+        load_words(f_word_table, f_words, slice(0, T))
 
-        picked = sbuf([P, 3 * V], U8, "picked")
-        e_cols, x_cols, f_cols = slice(0, V), slice(V, V + S), slice(V + S, 2 * V + S)
+        f_picked = sbuf([P, V], U8, "f_picked")
+        ex_picked = sbuf([P, V + S], U8, "ex_picked")
+        nc.vector.tensor_copy(f_picked[:], f_scale_table[:].indirect(cand_list[:]))
+        nc.vector.tensor_copy(ex_picked[:, 0:V], e_scale_table[:].indirect(cand_list[:]))
+        nc.vector.tensor_copy(ex_picked[:, V : V + S], x_scale_table[:].indirect(offs_list[:]))
 
-        def move_scale_rows(planes, cols):
+        def move_scale_rows(planes, picked):
             for r in range(4):
                 nc.sync.dma_start(
-                    out=planes[r:P:32, :].bitcast(I32), in_=picked[ROW_STEP * r : P : 32, cols].bitcast(I32)
+                    out=planes[r:P:32, :].bitcast(I32), in_=picked[32 + 4 * r : 96 : 16, :].bitcast(I32)
                 )
 
-        nc.vector.tensor_copy(picked[:, f_cols], f_scale_table[:].indirect(cand_list[:]))
-        nc.vector.tensor_copy(picked[:, e_cols], e_scale_table[:].indirect(cand_list[:]))
-        nc.vector.tensor_copy(picked[:, x_cols], x_scale_table[:].indirect(offs_list[:]))
-        move_scale_rows(f_plane, f_cols)
+        move_scale_rows(f_plane, f_picked)
+        x_word_table = sbuf([P, T], I32, "x_word_table", "f_scale_table")
         load_words(x_word_table, x_words, slice(0, T))
-        move_scale_rows(ex_planes, slice(0, V + S))
+        move_scale_rows(ex_planes, ex_picked)
+        h_raw.extend([placed([P, PACK, P], F32, f"h_late{u}", 2048 * u)[:] for u in range(2)])
+        load_h(1)
+        load_h(2)
 
         f_code = sbuf([P, V], U32, "f_code")
+        e_code = sbuf([P, V], U32, "e_code")
         x_code = sbuf([P, S], U32, "x_code")
-        h_code = sbuf([P, S], U32, "h_code", "x_scales_then_h_codes")
-        h_scale = sbuf([P, S], U8, "h_scale")
-        gather_words(f_code[:], f_word_table, cand_list[:])
-        for u in range(2):
-            users = slice(u * HALF, (u + 1) * HALF)
-            grouped = sbuf([P, HALF, PACK], BF16, f"grouped{u}")
-            nc.scalar.copy(out=grouped[:], in_=h_raw[:, :, users].rearrange("p j c -> p c j"))
+        h_code = [sbuf([P, c.stop - c.start], U32, f"h_code{i}") for i, c in enumerate(h_pieces)]
+        h_scale = [sbuf([P, c.stop - c.start], U8, f"h_scale{i}") for i, c in enumerate(h_pieces)]
+
+        def quantise_h(i):
+            grouped = sbuf([P, h_pieces[i].stop - h_pieces[i].start, PACK], BF16, f"grouped{i}")
+            nc.scalar.copy(out=grouped[:], in_=h_raw[i].rearrange("p j c -> p c j"))
             nc.vector.quantize_mx(
-                out=h_code[:, users].bitcast(FP8X4),
-                scales=h_scale[:, users],
-                in_=grouped[:].rearrange("p c j -> p (c j)"),
+                out=h_code[i][:].bitcast(FP8X4), scales=h_scale[i][:], in_=grouped[:].rearrange("p c j -> p (c j)")
             )
 
         scores = [psum.tile([P, V], F32, name=f"scores{t}") for t in range(TILES)]
-        for t in range(TILES):
-            users = slice(t * P, (t + 1) * P)
+
+        def session_pass(t, first):
+            i, cols = (0, slice(t * P, (t + 1) * P)) if t < 2 else (t - 1, slice(0, P))
             nc.tensor.matmul_mx(
                 out=scores[t][:],
-                lhsT=h_code[:, users].bitcast(FP8X4),
-                lhsT_scale=h_scale[:, users],
+                lhsT=h_code[i][:, cols].bitcast(FP8X4),
+                lhsT_scale=h_scale[i][:, cols],
                 rhs=f_code[:].bitcast(FP8X4),
                 rhs_scale=f_plane[:],
-                start=True,
-                stop=False,
+                start=first,
+                stop=not first,
             )
-        e_code = sbuf([P, V], U32, "e_code", "h_raw_then_e_codes")
-        gather_words(e_code[:], e_word_table, cand_list[:])
-        for u in range(2):
-            gather_words(x_code[:, u * HALF : (u + 1) * HALF], x_word_table, offs_list[:, u * HALF // 16 : (u + 1) * HALF // 16])
-        for t in range(TILES):
+
+        def user_pass(t, first):
             nc.tensor.matmul_mx(
                 out=scores[t][:],
                 lhsT=x_code[:, t * P : (t + 1) * P].bitcast(FP8X4),
                 lhsT_scale=ex_planes[:, V + t * P : V + (t + 1) * P],
                 rhs=e_code[:].bitcast(FP8X4),
-                rhs_scale=ex_planes[:, e_cols],
-                start=False,
-                stop=True,
+                rhs_scale=ex_planes[:, 0:V],
+                start=first,
+                stop=not first,
             )
 
-        weights = [sbuf([P, V], F32, f"weights{t}") for t in range(TILES)]
+        weights = [placed([P, V], F32, "weights0", 1024)] + [sbuf([P, V], F32, f"weights{t}") for t in range(1, TILES)]
         totals = [sbuf([P, 1], F32, f"total{t}") for t in range(TILES)]
+        inverses = [sbuf([P, 1], F32, f"inverse{t}") for t in range(TILES)]
 
         def exponentials(t):
-            neg_max = sbuf([P, 1], F32, f"neg_max{t}", "neg_max0" if t == 2 else None)
+            neg_max = placed([P, 1], F32, f"neg_max{t}", 4032 * t) if t < 2 else sbuf([P, 1], F32, f"neg_max{t}")
             nc.vector.tensor_reduce(neg_max[:], scores[t][:], mybir.AxisListType.X, ALU.max, negate=True)
             nc.scalar.activation(weights[t][:], scores[t][:], EXP, bias=neg_max[:], accum_out=totals[t][:])
 
         def normalise(t):
             rows = slice(t * P, (t + 1) * P)
-            inverse = sbuf([P, 1], F32, f"inverse{t}")
+            inverse = inverses[t]
             probs = sbuf([P, V], F32, f"probs{t}")
             nc.vector.reciprocal(inverse[:], totals[t][:])
             if t == 0:
-                nc.gpsimd.tensor_scalar(probs[:], weights[t][:], inverse[:], 1.0, ALU.mult, ALU.mult)
+                nc.gpsimd.tensor_scalar(probs[:], weights[t][:], inverse[:], 0.0, ALU.mult, ALU.add)
                 nc.sync.dma_start(out=out[rows, :], in_=probs[:])
             elif t < TILES - 1:
                 nc.vector.tensor_scalar(probs[:], weights[t][:], inverse[:], None, ALU.mult)
@@ -159,7 +168,22 @@ def tile_picked_zsess_soft_p_kernel(tc, x_words, x_scales, e_words, e_scales, f_
                 nc.scalar.activation(probs[:, right], weights[t][:, right], COPY, scale=inverse[:])
                 nc.scalar.dma_start(out=out[rows, right], in_=probs[:, right])
 
+        gather_words(e_code[:], e_word_table, cand_list[:])
+        quantise_h(0)
+        gather_words(f_code[:], f_word_table, cand_list[:])
+        session_pass(0, True)
+        session_pass(1, True)
+        for u in range(2):
+            gather_words(x_code[:, u * HALF : (u + 1) * HALF], x_word_table, offs_list[:, u * HALF // 16 : (u + 1) * HALF // 16])
+        user_pass(0, False)
+        user_pass(1, False)
+        quantise_h(1)
+        user_pass(2, True)
+        session_pass(2, False)
         exponentials(0)
+        quantise_h(2)
+        user_pass(3, True)
+        session_pass(3, False)
         exponentials(1)
         normalise(0)
         exponentials(2)

@@ -20,7 +20,8 @@ P = 128
 PACK = 4
 TILES = S // P
 HALF = S // 2
-FIRST_PIECE = 512
+FIRST_PIECE = 640
+FIRST_SPLIT = 256
 LAST_SPLIT = 320
 
 
@@ -73,8 +74,8 @@ def tile_picked_zsess_soft_p_kernel(tc, x_words, x_scales, e_words, e_scales, f_
         def load_h(i):
             nc.sync.dma_start(out=h_raw[i], in_=h_rows[:, :, h_pieces[i]])
 
-        nc.sync.dma_start(cand_list[:], cand)
         load_words(e_word_table, e_words, slice(0, FIRST_PIECE))
+        nc.sync.dma_start(cand_list[:], cand)
         load_scales(f_scale_table, f_scales)
         load_h(0)
         load_scales(e_scale_table, e_scales)
@@ -150,23 +151,16 @@ def tile_picked_zsess_soft_p_kernel(tc, x_words, x_scales, e_words, e_scales, f_
             nc.vector.tensor_reduce(neg_max[:], scores[t][:], mybir.AxisListType.X, ALU.max, negate=True)
             nc.scalar.activation(weights[t][:], scores[t][:], EXP, bias=neg_max[:], accum_out=totals[t][:])
 
-        def normalise(t):
-            rows = slice(t * P, (t + 1) * P)
-            inverse = inverses[t]
-            probs = sbuf([P, V], F32, f"probs{t}")
-            nc.vector.reciprocal(inverse[:], totals[t][:])
-            if t == 0:
-                nc.gpsimd.tensor_scalar(probs[:], weights[t][:], inverse[:], 0.0, ALU.mult, ALU.add)
-                nc.sync.dma_start(out=out[rows, :], in_=probs[:])
-            elif t < TILES - 1:
-                nc.vector.tensor_scalar(probs[:], weights[t][:], inverse[:], None, ALU.mult)
-                nc.sync.dma_start(out=out[rows, :], in_=probs[:])
-            else:
-                left, right = slice(0, LAST_SPLIT), slice(LAST_SPLIT, V)
-                nc.vector.tensor_scalar(probs[:, left], weights[t][:, left], inverse[:], None, ALU.mult)
-                nc.sync.dma_start(out=out[rows, left], in_=probs[:, left])
-                nc.scalar.activation(probs[:, right], weights[t][:, right], COPY, scale=inverse[:])
-                nc.scalar.dma_start(out=out[rows, right], in_=probs[:, right])
+        probs = [sbuf([P, V], F32, f"probs{t}") for t in range(TILES)]
+
+        def invert(t):
+            nc.vector.reciprocal(inverses[t][:], totals[t][:])
+
+        def scale_on_vector(t, cols):
+            nc.vector.tensor_scalar(probs[t][:, cols], weights[t][:, cols], inverses[t][:], None, ALU.mult)
+
+        def store(queue, t, cols):
+            queue.dma_start(out=out[t * P : (t + 1) * P, cols], in_=probs[t][:, cols])
 
         gather_words(e_code[:], e_word_table, cand_list[:])
         quantise_h(0)
@@ -185,8 +179,22 @@ def tile_picked_zsess_soft_p_kernel(tc, x_words, x_scales, e_words, e_scales, f_
         user_pass(3, True)
         session_pass(3, False)
         exponentials(1)
-        normalise(0)
         exponentials(2)
+        invert(0)
+        left, right = slice(0, FIRST_SPLIT), slice(FIRST_SPLIT, V)
+        nc.gpsimd.tensor_scalar(probs[0][:, left], weights[0][:, left], inverses[0][:], 0.0, ALU.mult, ALU.add)
         exponentials(3)
-        for t in range(1, TILES):
-            normalise(t)
+        invert(1)
+        scale_on_vector(0, right)
+        store(nc.sync, 0, slice(0, V))
+        scale_on_vector(1, slice(0, V))
+        store(nc.sync, 1, slice(0, V))
+        invert(2)
+        scale_on_vector(2, slice(0, V))
+        store(nc.sync, 2, slice(0, V))
+        invert(3)
+        left, right = slice(0, LAST_SPLIT), slice(LAST_SPLIT, V)
+        scale_on_vector(3, left)
+        store(nc.sync, 3, left)
+        nc.scalar.activation(probs[3][:, right], weights[3][:, right], COPY, scale=inverses[3][:])
+        store(nc.scalar, 3, right)

@@ -22,6 +22,7 @@ TILES = S // P
 HALF = S // 2
 FIRST_PIECE = 640
 FIRST_SPLIT = 256
+X_PIECE = 1536
 LAST_SPLIT = 320
 
 
@@ -53,16 +54,10 @@ def tile_picked_zsess_soft_p_kernel(tc, x_words, x_scales, e_words, e_scales, f_
         f_scale_table = sbuf([P, T], U8, "f_scale_table")
         e_scale_table = sbuf([P, T], U8, "e_scale_table")
         x_scale_table = placed([P, T], U8, "x_scale_table", 1024)
-        f_plane = sbuf([P, V], U8, "f_plane")
-        ex_planes = sbuf([P, V + S], U8, "ex_planes")
-        warm_in = sbuf([P, 1], F32, "warm_in")
-        warm_out = sbuf([P, 1], F32, "warm_out")
+        planes = sbuf([P, 2 * V + S], U8, "planes")
         for table in (f_scale_table, e_scale_table, x_scale_table):
             nc.vector.memset(table[:].bitcast(I32), 0)
-        nc.vector.memset(warm_in[:], 0.0)
-        nc.scalar.activation(warm_out[:], warm_in[:], EXP)
-        nc.vector.memset(f_plane[:].bitcast(I32), 0)
-        nc.vector.memset(ex_planes[:].bitcast(I32), 0)
+        nc.vector.memset(planes[:].bitcast(I32), 0)
 
         f_word_table = sbuf([P, T], I32, "f_word_table")
         e_word_table = sbuf([P, T], I32, "e_word_table")
@@ -78,28 +73,23 @@ def tile_picked_zsess_soft_p_kernel(tc, x_words, x_scales, e_words, e_scales, f_
         nc.sync.dma_start(cand_list[:], cand)
         load_scales(f_scale_table, f_scales)
         load_h(0)
-        load_scales(e_scale_table, e_scales)
         nc.sync.dma_start(offs_list[:], offs)
+        load_scales(e_scale_table, e_scales)
         load_scales(x_scale_table, x_scales)
         load_words(e_word_table, e_words, slice(FIRST_PIECE, T))
         load_words(f_word_table, f_words, slice(0, T))
 
-        f_picked = sbuf([P, V], U8, "f_picked")
-        ex_picked = sbuf([P, V + S], U8, "ex_picked")
-        nc.vector.tensor_copy(f_picked[:], f_scale_table[:].indirect(cand_list[:]))
-        nc.vector.tensor_copy(ex_picked[:, 0:V], e_scale_table[:].indirect(cand_list[:]))
-        nc.vector.tensor_copy(ex_picked[:, V : V + S], x_scale_table[:].indirect(offs_list[:]))
+        picked = sbuf([P, 2 * V + S], U8, "picked")
+        f_cols, e_cols, x_cols = slice(0, V), slice(V, 2 * V), slice(2 * V, 2 * V + S)
+        nc.vector.tensor_copy(picked[:, f_cols], f_scale_table[:].indirect(cand_list[:]))
+        nc.vector.tensor_copy(picked[:, e_cols], e_scale_table[:].indirect(cand_list[:]))
+        nc.vector.tensor_copy(picked[:, x_cols], x_scale_table[:].indirect(offs_list[:]))
 
-        def move_scale_rows(planes, picked):
-            for r in range(4):
-                nc.sync.dma_start(
-                    out=planes[r:P:32, :].bitcast(I32), in_=picked[32 + 4 * r : 96 : 16, :].bitcast(I32)
-                )
-
-        move_scale_rows(f_plane, f_picked)
-        x_word_table = sbuf([P, T], I32, "x_word_table", "f_scale_table")
-        load_words(x_word_table, x_words, slice(0, T))
-        move_scale_rows(ex_planes, ex_picked)
+        x_word_table = sbuf([P, T], I32, "x_word_table", "e_scale_table")
+        load_words(x_word_table, x_words, slice(0, X_PIECE))
+        for r in range(4):
+            nc.sync.dma_start(out=planes[r:P:32, :].bitcast(I32), in_=picked[32 + 4 * r : 96 : 16, :].bitcast(I32))
+        load_words(x_word_table, x_words, slice(X_PIECE, T))
         h_raw.extend([placed([P, PACK, P], F32, f"h_late{u}", 2048 * u)[:] for u in range(2)])
         load_h(1)
         load_h(2)
@@ -126,7 +116,7 @@ def tile_picked_zsess_soft_p_kernel(tc, x_words, x_scales, e_words, e_scales, f_
                 lhsT=h_code[i][:, cols].bitcast(FP8X4),
                 lhsT_scale=h_scale[i][:, cols],
                 rhs=f_code[:].bitcast(FP8X4),
-                rhs_scale=f_plane[:],
+                rhs_scale=planes[:, f_cols],
                 start=first,
                 stop=not first,
             )
@@ -135,9 +125,9 @@ def tile_picked_zsess_soft_p_kernel(tc, x_words, x_scales, e_words, e_scales, f_
             nc.tensor.matmul_mx(
                 out=scores[t][:],
                 lhsT=x_code[:, t * P : (t + 1) * P].bitcast(FP8X4),
-                lhsT_scale=ex_planes[:, V + t * P : V + (t + 1) * P],
+                lhsT_scale=planes[:, 2 * V + t * P : 2 * V + (t + 1) * P],
                 rhs=e_code[:].bitcast(FP8X4),
-                rhs_scale=ex_planes[:, 0:V],
+                rhs_scale=planes[:, e_cols],
                 start=first,
                 stop=not first,
             )

@@ -19,10 +19,8 @@ ALU = mybir.AluOpType
 P = 128
 PACK = 4
 TILES = S // P
-HALF = S // 2
-FIRST_PIECE = 640
-FIRST_SPLIT = 256
-X_PIECE = 1536
+F_CUTS = (0, 576, 1152, T)
+HALF_S = S // 2
 LAST_SPLIT = 320
 
 
@@ -30,14 +28,10 @@ def tile_picked_zsess_soft_p_kernel(tc, x_words, x_scales, e_words, e_scales, f_
     nc = tc.nc
     with ExitStack() as ctx:
         keep = ctx.enter_context(tc.tile_pool(name="keep", bufs=1))
-        reuse = ctx.enter_context(tc.tile_pool(name="reuse", bufs=1))
         psum = ctx.enter_context(tc.psum_pool(name="psum", bufs=1))
 
         def sbuf(shape, dtype, name, tag=None):
             return keep.tile(shape, dtype, name=name, tag=tag or name, align_bytes=64)
-
-        def placed(shape, dtype, name, offset):
-            return reuse.tile(shape, dtype, name=name, tag=name, align_bytes=64, offset=offset)
 
         def load_scales(table, scales):
             nc.sync.dma_start(out=table[32:96:4, :].bitcast(I32), in_=scales[0].bitcast(I32))
@@ -51,72 +45,73 @@ def tile_picked_zsess_soft_p_kernel(tc, x_words, x_scales, e_words, e_scales, f_
         cand_list = keep.tile([P, V // 16], U16)
         offs_list = keep.tile([P, S // 16], U16)
 
-        f_scale_table = sbuf([P, T], U8, "f_scale_table")
         e_scale_table = sbuf([P, T], U8, "e_scale_table")
-        x_scale_table = placed([P, T], U8, "x_scale_table", 1024)
-        planes = sbuf([P, 2 * V + S], U8, "planes")
+        x_scale_table = sbuf([P, T], U8, "x_scale_table")
+        f_scale_table = sbuf([P, T], U8, "f_scale_table")
+        f_plane = sbuf([P, V], U8, "f_plane")
+        planes = sbuf([P, V + S], U8, "planes")
         for table in (f_scale_table, e_scale_table, x_scale_table):
             nc.vector.memset(table[:].bitcast(I32), 0)
+        nc.vector.memset(f_plane[:].bitcast(I32), 0)
         nc.vector.memset(planes[:].bitcast(I32), 0)
 
-        f_word_table = sbuf([P, T], I32, "f_word_table")
         e_word_table = sbuf([P, T], I32, "e_word_table")
+        x_word_table = sbuf([P, T], I32, "x_word_table")
+        f_word_table = sbuf([P, T], I32, "f_word_table")
         h_rows = hT.rearrange("(p j) c -> p j c", j=PACK)
-        h_pieces = [slice(0, HALF), slice(HALF, HALF + P), slice(HALF + P, S)]
-        h_early = sbuf([P, PACK, HALF], F32, "h_early")
-        h_raw = [h_early[:]]
+        h_raw = sbuf([P, PACK, S], F32, "h_raw")
 
-        def load_h(i):
-            nc.sync.dma_start(out=h_raw[i], in_=h_rows[:, :, h_pieces[i]])
+        f_picked = sbuf([P, V], U8, "f_picked")
+        picked = sbuf([P, V + S], U8, "picked")
+        e_cols, x_cols = slice(0, V), slice(V, V + S)
 
-        load_words(e_word_table, e_words, slice(0, FIRST_PIECE))
+        def move_rows(plane, rows):
+            for r in range(4):
+                nc.sync.dma_start(out=plane[r:P:32, :].bitcast(I32), in_=rows[32 + 4 * r : 96 : 16, :].bitcast(I32))
+
+        load_words(f_word_table, f_words, slice(F_CUTS[0], F_CUTS[1]))
         nc.sync.dma_start(cand_list[:], cand)
         load_scales(f_scale_table, f_scales)
-        load_h(0)
+        load_words(f_word_table, f_words, slice(F_CUTS[1], F_CUTS[2]))
         nc.sync.dma_start(offs_list[:], offs)
         load_scales(e_scale_table, e_scales)
+        load_words(f_word_table, f_words, slice(F_CUTS[2], F_CUTS[3]))
         load_scales(x_scale_table, x_scales)
-        load_words(e_word_table, e_words, slice(FIRST_PIECE, T))
-        load_words(f_word_table, f_words, slice(0, T))
-
-        picked = sbuf([P, 2 * V + S], U8, "picked")
-        f_cols, e_cols, x_cols = slice(0, V), slice(V, 2 * V), slice(2 * V, 2 * V + S)
-        nc.vector.tensor_copy(picked[:, f_cols], f_scale_table[:].indirect(cand_list[:]))
+        nc.sync.dma_start(out=h_raw[:], in_=h_rows)
+        nc.vector.tensor_copy(f_picked[:], f_scale_table[:].indirect(cand_list[:]))
         nc.vector.tensor_copy(picked[:, e_cols], e_scale_table[:].indirect(cand_list[:]))
         nc.vector.tensor_copy(picked[:, x_cols], x_scale_table[:].indirect(offs_list[:]))
+        move_rows(f_plane, f_picked)
+        load_words(e_word_table, e_words, slice(0, T))
+        load_words(x_word_table, x_words, slice(0, T))
+        move_rows(planes, picked)
 
-        x_word_table = sbuf([P, T], I32, "x_word_table", "e_scale_table")
-        load_words(x_word_table, x_words, slice(0, X_PIECE))
-        for r in range(4):
-            nc.sync.dma_start(out=planes[r:P:32, :].bitcast(I32), in_=picked[32 + 4 * r : 96 : 16, :].bitcast(I32))
-        load_words(x_word_table, x_words, slice(X_PIECE, T))
-        h_raw.extend([placed([P, PACK, P], F32, f"h_late{u}", 2048 * u)[:] for u in range(2)])
-        load_h(1)
-        load_h(2)
-
-        f_code = sbuf([P, V], U32, "f_code")
         e_code = sbuf([P, V], U32, "e_code")
         x_code = sbuf([P, S], U32, "x_code")
-        h_code = [sbuf([P, c.stop - c.start], U32, f"h_code{i}") for i, c in enumerate(h_pieces)]
-        h_scale = [sbuf([P, c.stop - c.start], U8, f"h_scale{i}") for i, c in enumerate(h_pieces)]
+        f_code = sbuf([P, V], U32, "f_code", "x_scale_table")
+        grouped = [sbuf([P, HALF_S, PACK], BF16, f"grouped{i}") for i in range(2)]
+        h_scale = [sbuf([P, HALF_S], U8, f"h_scale{i}") for i in range(2)]
+        h_code = {}
 
-        def quantise_h(i):
-            grouped = sbuf([P, h_pieces[i].stop - h_pieces[i].start, PACK], BF16, f"grouped{i}")
-            nc.scalar.copy(out=grouped[:], in_=h_raw[i].rearrange("p j c -> p c j"))
+        def cast(i):
+            nc.scalar.copy(out=grouped[i][:], in_=h_raw[:, :, i * HALF_S : (i + 1) * HALF_S].rearrange("p j c -> p c j"))
+
+        def quantise(i, tag):
+            h_code[i] = sbuf([P, HALF_S], U32, f"h_code{i}", tag)
             nc.vector.quantize_mx(
-                out=h_code[i][:].bitcast(FP8X4), scales=h_scale[i][:], in_=grouped[:].rearrange("p c j -> p (c j)")
+                out=h_code[i][:].bitcast(FP8X4), scales=h_scale[i][:], in_=grouped[i][:].rearrange("p c j -> p (c j)")
             )
 
         scores = [psum.tile([P, V], F32, name=f"scores{t}") for t in range(TILES)]
 
         def session_pass(t, first):
-            i, cols = (0, slice(t * P, (t + 1) * P)) if t < 2 else (t - 1, slice(0, P))
+            i, cols = t // 2, slice(t % 2 * P, (t % 2 + 1) * P)
             nc.tensor.matmul_mx(
                 out=scores[t][:],
                 lhsT=h_code[i][:, cols].bitcast(FP8X4),
                 lhsT_scale=h_scale[i][:, cols],
                 rhs=f_code[:].bitcast(FP8X4),
-                rhs_scale=planes[:, f_cols],
+                rhs_scale=f_plane[:],
                 start=first,
                 stop=not first,
             )
@@ -125,23 +120,22 @@ def tile_picked_zsess_soft_p_kernel(tc, x_words, x_scales, e_words, e_scales, f_
             nc.tensor.matmul_mx(
                 out=scores[t][:],
                 lhsT=x_code[:, t * P : (t + 1) * P].bitcast(FP8X4),
-                lhsT_scale=planes[:, 2 * V + t * P : 2 * V + (t + 1) * P],
+                lhsT_scale=planes[:, V + t * P : V + (t + 1) * P],
                 rhs=e_code[:].bitcast(FP8X4),
                 rhs_scale=planes[:, e_cols],
                 start=first,
                 stop=not first,
             )
 
-        weights = [placed([P, V], F32, "weights0", 1024)] + [sbuf([P, V], F32, f"weights{t}") for t in range(1, TILES)]
+        weights = [sbuf([P, V], F32, f"weights{t}") for t in range(TILES)]
         totals = [sbuf([P, 1], F32, f"total{t}") for t in range(TILES)]
         inverses = [sbuf([P, 1], F32, f"inverse{t}") for t in range(TILES)]
+        probs = [sbuf([P, V], F32, f"probs{t}") for t in range(TILES)]
 
         def exponentials(t):
-            neg_max = placed([P, 1], F32, f"neg_max{t}", 4032 * t) if t < 2 else sbuf([P, 1], F32, f"neg_max{t}")
+            neg_max = sbuf([P, 1], F32, f"neg_max{t}", f"neg_max{t % 2}")
             nc.vector.tensor_reduce(neg_max[:], scores[t][:], mybir.AxisListType.X, ALU.max, negate=True)
             nc.scalar.activation(weights[t][:], scores[t][:], EXP, bias=neg_max[:], accum_out=totals[t][:])
-
-        probs = [sbuf([P, V], F32, f"probs{t}") for t in range(TILES)]
 
         def invert(t):
             nc.vector.reciprocal(inverses[t][:], totals[t][:])
@@ -149,34 +143,34 @@ def tile_picked_zsess_soft_p_kernel(tc, x_words, x_scales, e_words, e_scales, f_
         def scale_on_vector(t, cols):
             nc.vector.tensor_scalar(probs[t][:, cols], weights[t][:, cols], inverses[t][:], None, ALU.mult)
 
+        def scale_on_gpsimd(t, cols):
+            nc.gpsimd.tensor_scalar(probs[t][:, cols], weights[t][:, cols], inverses[t][:], 0.0, ALU.mult, ALU.add)
+
         def store(queue, t, cols):
             queue.dma_start(out=out[t * P : (t + 1) * P, cols], in_=probs[t][:, cols])
 
-        gather_words(e_code[:], e_word_table, cand_list[:])
-        quantise_h(0)
+        for i in range(2):
+            cast(i)
         gather_words(f_code[:], f_word_table, cand_list[:])
+        quantise(0, None)
         session_pass(0, True)
         session_pass(1, True)
+        gather_words(e_code[:], e_word_table, cand_list[:])
+        quantise(1, "e_word_table")
+        session_pass(2, True)
+        session_pass(3, True)
         for u in range(2):
-            gather_words(x_code[:, u * HALF : (u + 1) * HALF], x_word_table, offs_list[:, u * HALF // 16 : (u + 1) * HALF // 16])
-        user_pass(0, False)
-        user_pass(1, False)
-        quantise_h(1)
-        user_pass(2, True)
-        session_pass(2, False)
+            gather_words(x_code[:, u * HALF_S : (u + 1) * HALF_S], x_word_table, offs_list[:, u * HALF_S // 16 : (u + 1) * HALF_S // 16])
+        for t in range(TILES):
+            user_pass(t, False)
         exponentials(0)
-        quantise_h(2)
-        user_pass(3, True)
-        session_pass(3, False)
         exponentials(1)
-        exponentials(2)
         invert(0)
-        left, right = slice(0, FIRST_SPLIT), slice(FIRST_SPLIT, V)
-        nc.gpsimd.tensor_scalar(probs[0][:, left], weights[0][:, left], inverses[0][:], 0.0, ALU.mult, ALU.add)
-        exponentials(3)
-        invert(1)
-        scale_on_vector(0, right)
+        scale_on_gpsimd(0, slice(0, V))
         store(nc.sync, 0, slice(0, V))
+        exponentials(2)
+        invert(1)
+        exponentials(3)
         scale_on_vector(1, slice(0, V))
         store(nc.sync, 1, slice(0, V))
         invert(2)
@@ -185,6 +179,5 @@ def tile_picked_zsess_soft_p_kernel(tc, x_words, x_scales, e_words, e_scales, f_
         invert(3)
         left, right = slice(0, LAST_SPLIT), slice(LAST_SPLIT, V)
         scale_on_vector(3, left)
-        store(nc.sync, 3, left)
         nc.scalar.activation(probs[3][:, right], weights[3][:, right], COPY, scale=inverses[3][:])
-        store(nc.scalar, 3, right)
+        store(nc.sync, 3, slice(0, V))

@@ -19,9 +19,10 @@ ALU = mybir.AluOpType
 P = 128
 PACK = 4
 TILES = S // P
-F_CUTS = (0, 576, 1152, T)
+F_CUTS = (0, 512, 1024, T)
 HALF_S = S // 2
 LAST_SPLIT = 320
+FIRST_SPLIT = 256
 
 
 def tile_picked_zsess_soft_p_kernel(tc, x_words, x_scales, e_words, e_scales, f_words, f_scales, hT, offs, cand, out):
@@ -166,7 +167,8 @@ def tile_picked_zsess_soft_p_kernel(tc, x_words, x_scales, e_words, e_scales, f_
         exponentials(0)
         exponentials(1)
         invert(0)
-        scale_on_gpsimd(0, slice(0, V))
+        scale_on_gpsimd(0, slice(0, FIRST_SPLIT))
+        nc.scalar.activation(probs[0][:, FIRST_SPLIT:], weights[0][:, FIRST_SPLIT:], COPY, scale=inverses[0][:])
         store(nc.sync, 0, slice(0, V))
         exponentials(2)
         invert(1)

@@ -19,10 +19,9 @@ ALU = mybir.AluOpType
 P = 128
 PACK = 4
 TILES = S // P
-F_CUTS = (0, 512, 1024, T)
-HALF_S = S // 2
+HALF = S // 2
 LAST_SPLIT = 320
-FIRST_SPLIT = 256
+X_CUT = 768
 
 
 def tile_picked_zsess_soft_p_kernel(tc, x_words, x_scales, e_words, e_scales, f_words, f_scales, hT, offs, cand, out):
@@ -37,7 +36,7 @@ def tile_picked_zsess_soft_p_kernel(tc, x_words, x_scales, e_words, e_scales, f_
         def load_scales(table, scales):
             nc.sync.dma_start(out=table[32:96:4, :].bitcast(I32), in_=scales[0].bitcast(I32))
 
-        def load_words(table, words, cols):
+        def load_words(table, words, cols=slice(0, T)):
             nc.sync.dma_start(out=table[:, cols], in_=words[0].rearrange("p n t -> p (n t)").bitcast(I32)[:, cols])
 
         def gather_words(picked_words, table, entries):
@@ -49,97 +48,101 @@ def tile_picked_zsess_soft_p_kernel(tc, x_words, x_scales, e_words, e_scales, f_
         e_scale_table = sbuf([P, T], U8, "e_scale_table")
         x_scale_table = sbuf([P, T], U8, "x_scale_table")
         f_scale_table = sbuf([P, T], U8, "f_scale_table")
-        f_plane = sbuf([P, V], U8, "f_plane")
-        planes = sbuf([P, V + S], U8, "planes")
-        for table in (f_scale_table, e_scale_table, x_scale_table):
+        nc.gpsimd.memset(f_scale_table[:].bitcast(I32), 0)
+        for table in (e_scale_table, x_scale_table):
             nc.vector.memset(table[:].bitcast(I32), 0)
-        nc.vector.memset(f_plane[:].bitcast(I32), 0)
-        nc.vector.memset(planes[:].bitcast(I32), 0)
 
         e_word_table = sbuf([P, T], I32, "e_word_table")
-        x_word_table = sbuf([P, T], I32, "x_word_table")
         f_word_table = sbuf([P, T], I32, "f_word_table")
         h_rows = hT.rearrange("(p j) c -> p j c", j=PACK)
-        h_raw = sbuf([P, PACK, S], F32, "h_raw")
+        h_early = sbuf([P, PACK, HALF], F32, "h_early")
 
-        f_picked = sbuf([P, V], U8, "f_picked")
-        picked = sbuf([P, V + S], U8, "picked")
-        e_cols, x_cols = slice(0, V), slice(V, V + S)
+        picked = sbuf([P, 2 * V + S], U8, "picked")
+        planes = sbuf([P, 2 * V + S], U8, "planes")
+        f_cols, e_cols, x_cols = slice(0, V), slice(V, 2 * V), slice(2 * V, 2 * V + S)
+        nc.vector.memset(planes[:].bitcast(I32), 0)
 
-        def move_rows(plane, rows):
+        def place_rows(plane, rows):
             for r in range(4):
                 nc.sync.dma_start(out=plane[r:P:32, :].bitcast(I32), in_=rows[32 + 4 * r : 96 : 16, :].bitcast(I32))
 
-        load_words(f_word_table, f_words, slice(F_CUTS[0], F_CUTS[1]))
+        nc.sync.dma_start(out=h_early[:, 0:2, :], in_=h_rows[:, 0:2, 0:HALF])
         nc.sync.dma_start(cand_list[:], cand)
         load_scales(f_scale_table, f_scales)
-        load_words(f_word_table, f_words, slice(F_CUTS[1], F_CUTS[2]))
-        nc.sync.dma_start(offs_list[:], offs)
+        nc.sync.dma_start(out=h_early[:, 2:4, :], in_=h_rows[:, 2:4, 0:HALF])
         load_scales(e_scale_table, e_scales)
-        load_words(f_word_table, f_words, slice(F_CUTS[2], F_CUTS[3]))
+        nc.sync.dma_start(offs_list[:], offs)
         load_scales(x_scale_table, x_scales)
-        nc.sync.dma_start(out=h_raw[:], in_=h_rows)
-        nc.vector.tensor_copy(f_picked[:], f_scale_table[:].indirect(cand_list[:]))
+        load_words(f_word_table, f_words)
+        load_words(e_word_table, e_words)
+        x_word_table = sbuf([P, T], I32, "x_word_table")
+        load_words(x_word_table, x_words, slice(0, X_CUT))
+        nc.vector.tensor_copy(picked[:, f_cols], f_scale_table[:].indirect(cand_list[:]))
         nc.vector.tensor_copy(picked[:, e_cols], e_scale_table[:].indirect(cand_list[:]))
         nc.vector.tensor_copy(picked[:, x_cols], x_scale_table[:].indirect(offs_list[:]))
-        move_rows(f_plane, f_picked)
-        load_words(e_word_table, e_words, slice(0, T))
-        load_words(x_word_table, x_words, slice(0, T))
-        move_rows(planes, picked)
+        place_rows(planes, picked)
+        load_words(x_word_table, x_words, slice(X_CUT, T))
+        h_late = sbuf([P, PACK, HALF], F32, "h_late", "x_scale_table")
+        nc.sync.dma_start(out=h_late[:], in_=h_rows[:, :, HALF:S])
 
+        f_code = sbuf([P, V], U32, "f_code")
         e_code = sbuf([P, V], U32, "e_code")
-        x_code = sbuf([P, S], U32, "x_code")
-        f_code = sbuf([P, V], U32, "f_code", "x_scale_table")
-        grouped = [sbuf([P, HALF_S, PACK], BF16, f"grouped{i}") for i in range(2)]
-        h_scale = [sbuf([P, HALF_S], U8, f"h_scale{i}") for i in range(2)]
-        h_code = {}
-
-        def cast(i):
-            nc.scalar.copy(out=grouped[i][:], in_=h_raw[:, :, i * HALF_S : (i + 1) * HALF_S].rearrange("p j c -> p c j"))
-
-        def quantise(i, tag):
-            h_code[i] = sbuf([P, HALF_S], U32, f"h_code{i}", tag)
-            nc.vector.quantize_mx(
-                out=h_code[i][:].bitcast(FP8X4), scales=h_scale[i][:], in_=grouped[i][:].rearrange("p c j -> p (c j)")
-            )
-
+        x_first = sbuf([P, P], U32, "x_first")
+        x_middle = sbuf([P, 2 * P], U32, "x_middle")
+        x_code = {0: x_first[:], 1: x_middle[:, 0:P], 2: x_middle[:, P : 2 * P]}
+        early_grouped = sbuf([P, HALF, PACK], BF16, "early_grouped")
+        early_scale = sbuf([P, HALF], U8, "early_scale")
+        early_code = sbuf([P, HALF], U32, "early_code")
+        late_grouped = [sbuf([P, P, PACK], BF16, f"late_grouped{u}") for u in range(2)]
+        late_scale = [sbuf([P, P], U8, f"late_scale{u}") for u in range(2)]
+        late_code = [sbuf([P, P], U32, f"late_code{u}") for u in range(2)]
+        h_code = [early_code[:, 0:P], early_code[:, P:HALF], late_code[0][:], late_code[1][:]]
+        h_scale = [early_scale[:, 0:P], early_scale[:, P:HALF], late_scale[0][:], late_scale[1][:]]
         scores = [psum.tile([P, V], F32, name=f"scores{t}") for t in range(TILES)]
 
-        def session_pass(t, first):
-            i, cols = t // 2, slice(t % 2 * P, (t % 2 + 1) * P)
-            nc.tensor.matmul_mx(
-                out=scores[t][:],
-                lhsT=h_code[i][:, cols].bitcast(FP8X4),
-                lhsT_scale=h_scale[i][:, cols],
-                rhs=f_code[:].bitcast(FP8X4),
-                rhs_scale=f_plane[:],
-                start=first,
-                stop=not first,
-            )
+        def interleaved(grouped, raw):
+            return grouped.rearrange("p (c i) j -> p c j i", i=4), raw.rearrange("p j (c i) -> p c j i", i=4)
+
+        def quantise(code, scale, grouped):
+            nc.vector.quantize_mx(out=code.bitcast(FP8X4), scales=scale, in_=grouped.rearrange("p c j -> p (c j)"))
 
         def user_pass(t, first):
             nc.tensor.matmul_mx(
                 out=scores[t][:],
-                lhsT=x_code[:, t * P : (t + 1) * P].bitcast(FP8X4),
-                lhsT_scale=planes[:, V + t * P : V + (t + 1) * P],
+                lhsT=x_code[t].bitcast(FP8X4),
+                lhsT_scale=planes[:, 2 * V + t * P : 2 * V + (t + 1) * P],
                 rhs=e_code[:].bitcast(FP8X4),
                 rhs_scale=planes[:, e_cols],
                 start=first,
                 stop=not first,
             )
 
+        def session_pass(t, first):
+            nc.tensor.matmul_mx(
+                out=scores[t][:],
+                lhsT=h_code[t].bitcast(FP8X4),
+                lhsT_scale=h_scale[t],
+                rhs=f_code[:].bitcast(FP8X4),
+                rhs_scale=planes[:, f_cols],
+                start=first,
+                stop=not first,
+            )
+
         weights = [sbuf([P, V], F32, f"weights{t}") for t in range(TILES)]
-        totals = [sbuf([P, 1], F32, f"total{t}") for t in range(TILES)]
+        totals = [h_late[:, 0, 0:1]] + [sbuf([P, 1], F32, f"total{t}")[:] for t in range(1, TILES)]
         inverses = [sbuf([P, 1], F32, f"inverse{t}") for t in range(TILES)]
         probs = [sbuf([P, V], F32, f"probs{t}") for t in range(TILES)]
+        first_max = sbuf([P, 1], F32, "first_max")
+        neg_max = [first_max[:], h_late[:, 1, P : P + 1]] * 2
+
+        def maximum(t):
+            nc.vector.tensor_reduce(neg_max[t], scores[t][:], mybir.AxisListType.X, ALU.max, negate=True)
 
         def exponentials(t):
-            neg_max = sbuf([P, 1], F32, f"neg_max{t}", f"neg_max{t % 2}")
-            nc.vector.tensor_reduce(neg_max[:], scores[t][:], mybir.AxisListType.X, ALU.max, negate=True)
-            nc.scalar.activation(weights[t][:], scores[t][:], EXP, bias=neg_max[:], accum_out=totals[t][:])
+            nc.scalar.activation(weights[t][:], scores[t][:], EXP, bias=neg_max[t], accum_out=totals[t])
 
         def invert(t):
-            nc.vector.reciprocal(inverses[t][:], totals[t][:])
+            nc.vector.reciprocal(inverses[t][:], totals[t])
 
         def scale_on_vector(t, cols):
             nc.vector.tensor_scalar(probs[t][:, cols], weights[t][:, cols], inverses[t][:], None, ALU.mult)
@@ -147,39 +150,50 @@ def tile_picked_zsess_soft_p_kernel(tc, x_words, x_scales, e_words, e_scales, f_
         def scale_on_gpsimd(t, cols):
             nc.gpsimd.tensor_scalar(probs[t][:, cols], weights[t][:, cols], inverses[t][:], 0.0, ALU.mult, ALU.add)
 
-        def store(queue, t, cols):
-            queue.dma_start(out=out[t * P : (t + 1) * P, cols], in_=probs[t][:, cols])
+        def store(t):
+            nc.sync.dma_start(out=out[t * P : (t + 1) * P, :], in_=probs[t][:])
 
-        for i in range(2):
-            cast(i)
+        whole = slice(0, V)
+        nc.scalar.copy(*interleaved(early_grouped[:], h_early[:]))
         gather_words(f_code[:], f_word_table, cand_list[:])
-        quantise(0, None)
+        quantise(early_code[:], early_scale[:], early_grouped[:])
+        gather_words(e_code[:], e_word_table, cand_list[:])
         session_pass(0, True)
         session_pass(1, True)
-        gather_words(e_code[:], e_word_table, cand_list[:])
-        quantise(1, "e_word_table")
-        session_pass(2, True)
-        session_pass(3, True)
-        for u in range(2):
-            gather_words(x_code[:, u * HALF_S : (u + 1) * HALF_S], x_word_table, offs_list[:, u * HALF_S // 16 : (u + 1) * HALF_S // 16])
-        for t in range(TILES):
-            user_pass(t, False)
+        gather_words(x_first[:], x_word_table, offs_list[:, 0 : P // 16])
+        for t in (1, 2):
+            gather_words(x_code[t], x_word_table, offs_list[:, t * P // 16 : (t + 1) * P // 16])
+        for t in range(3):
+            user_pass(t, t >= 2)
+        maximum(0)
+        x_last = sbuf([P, P], U32, "x_last")
+        x_code[3] = x_last[:]
+        gather_words(x_last[:], x_word_table, offs_list[:, 3 * P // 16 : S // 16])
+        user_pass(3, True)
+        nc.gpsimd.tensor_scalar(late_grouped[1][:], h_late[:, :, P:HALF].rearrange("p j c -> p c j"), 1.0, 0.0, ALU.mult, ALU.add)
+        nc.scalar.copy(*interleaved(late_grouped[0][:], h_late[:, :, 0:P]))
         exponentials(0)
+        for u in range(2):
+            quantise(late_code[u][:], late_scale[u][:], late_grouped[u][:])
+        for u in range(2):
+            session_pass(2 + u, False)
+        maximum(1)
         exponentials(1)
         invert(0)
-        scale_on_gpsimd(0, slice(0, FIRST_SPLIT))
-        nc.scalar.activation(probs[0][:, FIRST_SPLIT:], weights[0][:, FIRST_SPLIT:], COPY, scale=inverses[0][:])
-        store(nc.sync, 0, slice(0, V))
+        scale_on_gpsimd(0, whole)
+        store(0)
+        maximum(2)
         exponentials(2)
         invert(1)
+        maximum(3)
         exponentials(3)
-        scale_on_vector(1, slice(0, V))
-        store(nc.sync, 1, slice(0, V))
+        scale_on_vector(1, whole)
+        store(1)
         invert(2)
-        scale_on_vector(2, slice(0, V))
-        store(nc.sync, 2, slice(0, V))
+        scale_on_vector(2, whole)
+        store(2)
         invert(3)
         left, right = slice(0, LAST_SPLIT), slice(LAST_SPLIT, V)
         scale_on_vector(3, left)
         nc.scalar.activation(probs[3][:, right], weights[3][:, right], COPY, scale=inverses[3][:])
-        store(nc.sync, 3, slice(0, V))
+        store(3)

@@ -92,7 +92,7 @@ def tile_picked_zsess_soft_p_kernel(tc, x_words, x_scales, e_words, e_scales, f_
         x_code = {0: x_first[:], 1: x_middle[:, 0:P], 2: x_middle[:, P : 2 * P]}
         early_grouped = sbuf([P, HALF, PACK], BF16, "early_grouped")
         early_scale = sbuf([P, HALF], U8, "early_scale")
-        early_code = sbuf([P, HALF], U32, "early_code")
+        early_code = sbuf([P, HALF], U32, "early_code", "f_word_table")
         late_grouped = [sbuf([P, P, PACK], BF16, f"late_grouped{u}") for u in range(2)]
         late_scale = [sbuf([P, P], U8, f"late_scale{u}") for u in range(2)]
         late_code = [sbuf([P, P], U32, f"late_code{u}") for u in range(2)]
@@ -157,6 +157,17 @@ def tile_picked_zsess_soft_p_kernel(tc, x_words, x_scales, e_words, e_scales, f_
         nc.scalar.copy(*interleaved(early_grouped[:], h_early[:]))
         gather_words(f_code[:], f_word_table, cand_list[:])
         quantise(early_code[:], early_scale[:], early_grouped[:])
+        unread = psum.tile([P, V], F32, name="unread")
+        for cols, lo in ((slice(0, HALF), 0), (slice(0, P), HALF)):
+            nc.tensor.matmul_mx(
+                out=unread[:, lo : lo + cols.stop],
+                lhsT=h_code[0].bitcast(FP8X4),
+                lhsT_scale=h_scale[0],
+                rhs=early_code[:, cols].bitcast(FP8X4),
+                rhs_scale=early_scale[:, cols],
+                start=True,
+                stop=True,
+            )
         gather_words(e_code[:], e_word_table, cand_list[:])
         session_pass(0, True)
         session_pass(1, True)

@@ -22,6 +22,7 @@ TILES = S // P
 HALF = S // 2
 LAST_SPLIT = 320
 X_CUT = 768
+POOL_CAST = 64
 
 
 def tile_picked_zsess_soft_p_kernel(tc, x_words, x_scales, e_words, e_scales, f_words, f_scales, hT, offs, cand, out):
@@ -129,11 +130,11 @@ def tile_picked_zsess_soft_p_kernel(tc, x_words, x_scales, e_words, e_scales, f_
             )
 
         weights = [sbuf([P, V], F32, f"weights{t}") for t in range(TILES)]
-        totals = [h_late[:, 0, 0:1]] + [sbuf([P, 1], F32, f"total{t}")[:] for t in range(1, TILES)]
+        totals = [h_late[:, 0, HALF - 1 : HALF]] + [sbuf([P, 1], F32, f"total{t}")[:] for t in range(1, TILES)]
         inverses = [sbuf([P, 1], F32, f"inverse{t}") for t in range(TILES)]
         probs = [sbuf([P, V], F32, f"probs{t}") for t in range(TILES)]
         first_max = sbuf([P, 1], F32, "first_max")
-        neg_max = [first_max[:], h_late[:, 1, P : P + 1]] * 2
+        neg_max = [first_max[:], h_late[:, 1, 0:1]] * 2
 
         def maximum(t):
             nc.vector.tensor_reduce(neg_max[t], scores[t][:], mybir.AxisListType.X, ALU.max, negate=True)
@@ -181,15 +182,16 @@ def tile_picked_zsess_soft_p_kernel(tc, x_words, x_scales, e_words, e_scales, f_
         x_code[3] = x_last[:]
         gather_words(x_last[:], x_word_table, offs_list[:, 3 * P // 16 : S // 16])
         user_pass(3, True)
-        nc.gpsimd.tensor_scalar(late_grouped[1][:], h_late[:, :, P:HALF].rearrange("p j c -> p c j"), 1.0, 0.0, ALU.mult, ALU.add)
+        nc.gpsimd.tensor_scalar(late_grouped[1][:, 0:POOL_CAST], h_late[:, :, P : P + POOL_CAST].rearrange("p j c -> p c j"), 1.0, 0.0, ALU.mult, ALU.add)
         nc.scalar.copy(*interleaved(late_grouped[0][:], h_late[:, :, 0:P]))
+        nc.scalar.copy(*interleaved(late_grouped[1][:, POOL_CAST:P], h_late[:, :, P + POOL_CAST : HALF]))
         exponentials(0)
-        for u in range(2):
-            quantise(late_code[u][:], late_scale[u][:], late_grouped[u][:])
-        for u in range(2):
-            session_pass(2 + u, False)
+        quantise(late_code[0][:], late_scale[0][:], late_grouped[0][:])
+        session_pass(2, False)
         maximum(1)
         exponentials(1)
+        quantise(late_code[1][:], late_scale[1][:], late_grouped[1][:])
+        session_pass(3, False)
         invert(0)
         scale_on_gpsimd(0, whole)
         store(0)

@@ -22,7 +22,7 @@ TILES = S // P
 HALF = S // 2
 LAST_SPLIT = 320
 X_CUT = 768
-POOL_CAST = 64
+VECTOR_CAST = 48
 
 
 def tile_picked_zsess_soft_p_kernel(tc, x_words, x_scales, e_words, e_scales, f_words, f_scales, hT, offs, cand, out):
@@ -83,8 +83,9 @@ def tile_picked_zsess_soft_p_kernel(tc, x_words, x_scales, e_words, e_scales, f_
         nc.vector.tensor_copy(picked[:, x_cols], x_scale_table[:].indirect(offs_list[:]))
         place_rows(planes, picked)
         load_words(x_word_table, x_words, slice(X_CUT, T))
-        h_late = sbuf([P, PACK, HALF], F32, "h_late", "x_scale_table")
-        nc.sync.dma_start(out=h_late[:], in_=h_rows[:, :, HALF:S])
+        h_late = [sbuf([P, PACK, P], F32, f"h_late{u}", ("x_scale_table", "e_scale_table")[u]) for u in range(2)]
+        for u in range(2):
+            nc.sync.dma_start(out=h_late[u][:], in_=h_rows[:, :, HALF + u * P : HALF + (u + 1) * P])
 
         f_code = sbuf([P, V], U32, "f_code")
         e_code = sbuf([P, V], U32, "e_code")
@@ -130,11 +131,11 @@ def tile_picked_zsess_soft_p_kernel(tc, x_words, x_scales, e_words, e_scales, f_
             )
 
         weights = [sbuf([P, V], F32, f"weights{t}") for t in range(TILES)]
-        totals = [h_late[:, 0, HALF - 1 : HALF]] + [sbuf([P, 1], F32, f"total{t}")[:] for t in range(1, TILES)]
+        totals = [h_late[1][:, 0, P - 1 : P]] + [sbuf([P, 1], F32, f"total{t}")[:] for t in range(1, TILES)]
         inverses = [sbuf([P, 1], F32, f"inverse{t}") for t in range(TILES)]
         probs = [sbuf([P, V], F32, f"probs{t}") for t in range(TILES)]
         first_max = sbuf([P, 1], F32, "first_max")
-        neg_max = [first_max[:], h_late[:, 1, 0:1]] * 2
+        neg_max = [first_max[:], h_late[1][:, 1, P - 1 : P]] * 2
 
         def maximum(t):
             nc.vector.tensor_reduce(neg_max[t], scores[t][:], mybir.AxisListType.X, ALU.max, negate=True)
@@ -182,11 +183,11 @@ def tile_picked_zsess_soft_p_kernel(tc, x_words, x_scales, e_words, e_scales, f_
         x_code[3] = x_last[:]
         gather_words(x_last[:], x_word_table, offs_list[:, 3 * P // 16 : S // 16])
         user_pass(3, True)
-        nc.gpsimd.tensor_scalar(late_grouped[1][:, 0:POOL_CAST], h_late[:, :, P : P + POOL_CAST].rearrange("p j c -> p c j"), 1.0, 0.0, ALU.mult, ALU.add)
-        nc.scalar.copy(*interleaved(late_grouped[0][:], h_late[:, :, 0:P]))
-        nc.scalar.copy(*interleaved(late_grouped[1][:, POOL_CAST:P], h_late[:, :, P + POOL_CAST : HALF]))
+        nc.scalar.copy(*interleaved(late_grouped[0][:], h_late[0][:]))
+        nc.scalar.copy(*interleaved(late_grouped[1][:, VECTOR_CAST:P], h_late[1][:, :, VECTOR_CAST:P]))
         exponentials(0)
         quantise(late_code[0][:], late_scale[0][:], late_grouped[0][:])
+        nc.vector.tensor_copy(*interleaved(late_grouped[1][:, 0:VECTOR_CAST], h_late[1][:, :, 0:VECTOR_CAST]))
         session_pass(2, False)
         maximum(1)
         exponentials(1)

@@ -20,6 +20,7 @@ P = 128
 PACK = 4
 TILES = S // P
 HALF = S // 2
+FIRST_SPLIT = 352
 LAST_SPLIT = 320
 X_CUT = 768
 VECTOR_CAST = 48
@@ -194,7 +195,8 @@ def tile_picked_zsess_soft_p_kernel(tc, x_words, x_scales, e_words, e_scales, f_
         quantise(late_code[1][:], late_scale[1][:], late_grouped[1][:])
         session_pass(3, False)
         invert(0)
-        scale_on_gpsimd(0, whole)
+        scale_on_gpsimd(0, slice(0, FIRST_SPLIT))
+        nc.scalar.activation(probs[0][:, FIRST_SPLIT:V], weights[0][:, FIRST_SPLIT:V], COPY, scale=inverses[0][:])
         store(0)
         maximum(2)
         exponentials(2)

from contextlib import ExitStack

import concourse.mybir as mybir

K, T, S, V = 512, 2048, 512, 512
FLOPS = 2 * 2 * K * S * V

F32 = mybir.dt.float32
BF16 = mybir.dt.bfloat16
I32 = mybir.dt.int32
U32 = mybir.dt.uint32
U16 = mybir.dt.uint16
U8 = mybir.dt.uint8
FP8X4 = mybir.dt.float8_e4m3fn_x4
EXP = mybir.ActivationFunctionType.Exp
COPY = mybir.ActivationFunctionType.Copy
ALU = mybir.AluOpType

P = 128
PACK = 4
TILES = S // P
HALF = S // 2
FIRST_SPLIT = 352
LAST_SPLIT = 320
X_CUT = 768
VECTOR_CAST = 48


def tile_picked_zsess_soft_p_kernel(tc, x_words, x_scales, e_words, e_scales, f_words, f_scales, hT, offs, cand, out):
    nc = tc.nc
    with ExitStack() as ctx:
        keep = ctx.enter_context(tc.tile_pool(name="keep", bufs=1))
        psum = ctx.enter_context(tc.psum_pool(name="psum", bufs=1))

        def sbuf(shape, dtype, name, tag=None):
            return keep.tile(shape, dtype, name=name, tag=tag or name, align_bytes=64)

        def load_scales(table, scales):
            nc.sync.dma_start(out=table[32:96:4, :].bitcast(I32), in_=scales[0].bitcast(I32))

        def load_words(table, words, cols=slice(0, T)):
            nc.sync.dma_start(out=table[:, cols], in_=words[0].rearrange("p n t -> p (n t)").bitcast(I32)[:, cols])

        def gather_words(picked_words, table, entries):
            nc.vector.tensor_copy(picked_words, table[:].bitcast(U32).indirect(entries))

        cand_list = keep.tile([P, V // 16], U16)
        offs_list = keep.tile([P, S // 16], U16)

        e_scale_table = sbuf([P, T], U8, "e_scale_table")
        x_scale_table = sbuf([P, T], U8, "x_scale_table")
        f_scale_table = sbuf([P, T], U8, "f_scale_table")
        nc.gpsimd.memset(f_scale_table[:].bitcast(I32), 0)
        for table in (e_scale_table, x_scale_table):
            nc.vector.memset(table[:].bitcast(I32), 0)

        e_word_table = sbuf([P, T], I32, "e_word_table")
        f_word_table = sbuf([P, T], I32, "f_word_table")
        h_rows = hT.rearrange("(p j) c -> p j c", j=PACK)
        h_early = sbuf([P, PACK, HALF], F32, "h_early")

        picked = sbuf([P, 2 * V + S], U8, "picked")
        planes = sbuf([P, 2 * V + S], U8, "planes")
        f_cols, e_cols, x_cols = slice(0, V), slice(V, 2 * V), slice(2 * V, 2 * V + S)
        nc.vector.memset(planes[:].bitcast(I32), 0)

        def place_rows(plane, rows):
            for r in range(4):
                nc.sync.dma_start(out=plane[r:P:32, :].bitcast(I32), in_=rows[32 + 4 * r : 96 : 16, :].bitcast(I32))

        nc.sync.dma_start(out=h_early[:, 0:2, :], in_=h_rows[:, 0:2, 0:HALF])
        nc.sync.dma_start(cand_list[:], cand)
        load_scales(f_scale_table, f_scales)
        nc.sync.dma_start(out=h_early[:, 2:4, :], in_=h_rows[:, 2:4, 0:HALF])
        load_scales(e_scale_table, e_scales)
        nc.sync.dma_start(offs_list[:], offs)
        load_scales(x_scale_table, x_scales)
        load_words(f_word_table, f_words)
        load_words(e_word_table, e_words)
        x_word_table = sbuf([P, T], I32, "x_word_table")
        load_words(x_word_table, x_words, slice(0, X_CUT))
        nc.vector.tensor_copy(picked[:, f_cols], f_scale_table[:].indirect(cand_list[:]))
        nc.vector.tensor_copy(picked[:, e_cols], e_scale_table[:].indirect(cand_list[:]))
        nc.vector.tensor_copy(picked[:, x_cols], x_scale_table[:].indirect(offs_list[:]))
        place_rows(planes, picked)
        load_words(x_word_table, x_words, slice(X_CUT, T))
        h_late = [sbuf([P, PACK, P], F32, f"h_late{u}", ("x_scale_table", "e_scale_table")[u]) for u in range(2)]
        for u in range(2):
            nc.sync.dma_start(out=h_late[u][:], in_=h_rows[:, :, HALF + u * P : HALF + (u + 1) * P])

        f_code = sbuf([P, V], U32, "f_code")
        e_code = sbuf([P, V], U32, "e_code")
        x_first = sbuf([P, P], U32, "x_first")
        x_middle = sbuf([P, 2 * P], U32, "x_middle")
        x_code = {0: x_first[:], 1: x_middle[:, 0:P], 2: x_middle[:, P : 2 * P]}
        early_grouped = sbuf([P, HALF, PACK], BF16, "early_grouped")
        early_scale = sbuf([P, HALF], U8, "early_scale")
        early_code = sbuf([P, HALF], U32, "early_code", "f_word_table")
        late_grouped = [sbuf([P, P, PACK], BF16, f"late_grouped{u}") for u in range(2)]
        late_scale = [sbuf([P, P], U8, f"late_scale{u}") for u in range(2)]
        late_code = [sbuf([P, P], U32, f"late_code{u}") for u in range(2)]
        h_code = [early_code[:, 0:P], early_code[:, P:HALF], late_code[0][:], late_code[1][:]]
        h_scale = [early_scale[:, 0:P], early_scale[:, P:HALF], late_scale[0][:], late_scale[1][:]]
        scores = [psum.tile([P, V], F32, name=f"scores{t}") for t in range(TILES)]

        def interleaved(grouped, raw):
            return grouped.rearrange("p (c i) j -> p c j i", i=4), raw.rearrange("p j (c i) -> p c j i", i=4)

        def quantise(code, scale, grouped):
            nc.vector.quantize_mx(out=code.bitcast(FP8X4), scales=scale, in_=grouped.rearrange("p c j -> p (c j)"))

        def user_pass(t, first):
            nc.tensor.matmul_mx(
                out=scores[t][:],
                lhsT=x_code[t].bitcast(FP8X4),
                lhsT_scale=planes[:, 2 * V + t * P : 2 * V + (t + 1) * P],
                rhs=e_code[:].bitcast(FP8X4),
                rhs_scale=planes[:, e_cols],
                start=first,
                stop=not first,
            )

        def session_pass(t, first):
            nc.tensor.matmul_mx(
                out=scores[t][:],
                lhsT=h_code[t].bitcast(FP8X4),
                lhsT_scale=h_scale[t],
                rhs=f_code[:].bitcast(FP8X4),
                rhs_scale=planes[:, f_cols],
                start=first,
                stop=not first,
            )

        weights = [sbuf([P, V], F32, f"weights{t}") for t in range(TILES)]
        totals = [h_late[1][:, 0, P - 1 : P]] + [sbuf([P, 1], F32, f"total{t}")[:] for t in range(1, TILES)]
        inverses = [sbuf([P, 1], F32, f"inverse{t}") for t in range(TILES)]
        probs = [sbuf([P, V], F32, f"probs{t}") for t in range(TILES)]
        first_max = sbuf([P, 1], F32, "first_max")
        neg_max = [first_max[:], h_late[1][:, 1, P - 1 : P]] * 2

        def maximum(t):
            nc.vector.tensor_reduce(neg_max[t], scores[t][:], mybir.AxisListType.X, ALU.max, negate=True)

        def exponentials(t):
            nc.scalar.activation(weights[t][:], scores[t][:], EXP, bias=neg_max[t], accum_out=totals[t])

        def invert(t):
            nc.vector.reciprocal(inverses[t][:], totals[t])

        def scale_on_vector(t, cols):
            nc.vector.tensor_scalar(probs[t][:, cols], weights[t][:, cols], inverses[t][:], None, ALU.mult)

        def scale_on_gpsimd(t, cols):
            nc.gpsimd.tensor_scalar(probs[t][:, cols], weights[t][:, cols], inverses[t][:], 0.0, ALU.mult, ALU.add)

        def store(t):
            nc.sync.dma_start(out=out[t * P : (t + 1) * P, :], in_=probs[t][:])

        whole = slice(0, V)
        nc.scalar.copy(*interleaved(early_grouped[:], h_early[:]))
        gather_words(f_code[:], f_word_table, cand_list[:])
        quantise(early_code[:], early_scale[:], early_grouped[:])
        unread = psum.tile([P, V], F32, name="unread")
        for cols, lo in ((slice(0, HALF), 0), (slice(0, P), HALF)):
            nc.tensor.matmul_mx(
                out=unread[:, lo : lo + cols.stop],
                lhsT=h_code[0].bitcast(FP8X4),
                lhsT_scale=h_scale[0],
                rhs=early_code[:, cols].bitcast(FP8X4),
                rhs_scale=early_scale[:, cols],
                start=True,
                stop=True,
            )
        gather_words(e_code[:], e_word_table, cand_list[:])
        session_pass(0, True)
        session_pass(1, True)
        gather_words(x_first[:], x_word_table, offs_list[:, 0 : P // 16])
        for t in (1, 2):
            gather_words(x_code[t], x_word_table, offs_list[:, t * P // 16 : (t + 1) * P // 16])
        for t in range(3):
            user_pass(t, t >= 2)
        maximum(0)
        x_last = sbuf([P, P], U32, "x_last")
        x_code[3] = x_last[:]
        gather_words(x_last[:], x_word_table, offs_list[:, 3 * P // 16 : S // 16])
        user_pass(3, True)
        nc.scalar.copy(*interleaved(late_grouped[0][:], h_late[0][:]))
        nc.scalar.copy(*interleaved(late_grouped[1][:, VECTOR_CAST:P], h_late[1][:, :, VECTOR_CAST:P]))
        exponentials(0)
        quantise(late_code[0][:], late_scale[0][:], late_grouped[0][:])
        nc.vector.tensor_copy(*interleaved(late_grouped[1][:, 0:VECTOR_CAST], h_late[1][:, :, 0:VECTOR_CAST]))
        session_pass(2, False)
        maximum(1)
        exponentials(1)
        quantise(late_code[1][:], late_scale[1][:], late_grouped[1][:])
        session_pass(3, False)
        invert(0)
        scale_on_gpsimd(0, slice(0, FIRST_SPLIT))
        nc.scalar.activation(probs[0][:, FIRST_SPLIT:V], weights[0][:, FIRST_SPLIT:V], COPY, scale=inverses[0][:])
        store(0)
        maximum(2)
        exponentials(2)
        invert(1)
        maximum(3)
        exponentials(3)
        scale_on_vector(1, whole)
        store(1)
        invert(2)
        scale_on_vector(2, whole)
        store(2)
        invert(3)
        left, right = slice(0, LAST_SPLIT), slice(LAST_SPLIT, V)
        scale_on_vector(3, left)
        nc.scalar.activation(probs[3][:, right], weights[3][:, right], COPY, scale=inverses[3][:])
        store(3)
